import numpy as np
import ml_dtypes


def mxq(x, axis, fmt="e4m3"):
    dtype, down = {"e4m3": (ml_dtypes.float8_e4m3fn, 7), "e5m2": (ml_dtypes.float8_e5m2, 14)}[fmt]
    v = np.moveaxis(np.asarray(x, np.float32).astype(ml_dtypes.bfloat16).astype(np.float64), axis, -1)
    blocks = v.reshape(v.shape[:-1] + (-1, 32))
    amax = np.abs(blocks).max(-1, keepdims=True)
    byte = np.maximum(np.where(amax > 0, np.frexp(amax)[1] - 1 + 127, 0) - down, 1)
    scale = np.exp2(byte - 127.0)
    codes = (blocks / scale).astype(np.float32).astype(dtype).astype(np.float64)
    return np.moveaxis((codes * scale).reshape(v.shape), -1, axis)


WIDE = False


def mx_kscale(k):
    if not WIDE:
        return np.ones(k)
    levels = np.array([10, -10, 5, -5, 0])
    if k % 512:
        return np.exp2(np.random.permutation(np.resize(levels, k // 32))).repeat(32)
    a = np.empty((k // 512, 16))
    for p in range(k // 512):
        a[p, :8] = np.random.permutation(np.resize(levels, 8))
        for g in range(8):
            far = levels[np.abs(levels - a[p, g]) >= 10]
            a[p, g + 8] = far[np.random.randint(len(far))]
    return np.exp2(a.ravel()).repeat(32)


def f64(x):
    return np.asarray(x).astype(np.float64)


def striped(idx):
    return np.tile(idx.reshape(-1, 16).T, (8, 1)).astype(np.uint16)


def unstriped(offs):
    return offs[:16].T.reshape(-1).astype(np.int64)


E2M1 = np.array([0.0, 0.5, 1.0, 1.5, 2.0, 3.0, 4.0, 6.0, -0.0, -0.5, -1.0, -1.5, -2.0, -3.0, -4.0, -6.0])


def pack_weight(w, fmt):
    k, n = w.shape
    w = f64(np.asarray(w, np.float32).astype(ml_dtypes.bfloat16)).reshape(k // 32, 32, n)
    amax = np.abs(w).max(1)
    if fmt == "e4m3":
        byte = np.frexp(amax)[1] - 1 + 127 - 7
    else:
        mant, ex = np.frexp(amax / 6.0)
        byte = np.where(mant > 0.5, ex, ex - 1) + 127
    byte = np.clip(np.where(amax > 0, byte, 1), 1, 254)
    scaled = (w * np.exp2(127.0 - byte)[:, None, :]).reshape(k, n).astype(np.float32)
    by_word = np.ascontiguousarray(scaled.reshape(k // 512, 128, 4, n).transpose(0, 1, 3, 2))
    if fmt == "e4m3":
        words = by_word.astype(ml_dtypes.float8_e4m3fn).view(np.uint8)
    else:
        c = by_word.astype(ml_dtypes.float4_e2m1fn).view(np.uint8) & 0xF
        words = (c[..., 0::2] | (c[..., 1::2] << 4)).reshape(k // 512, 128, 2 * n)
    return np.ascontiguousarray(words), np.ascontiguousarray(byte.astype(np.uint8).reshape(k // 512, 16, n))


def unpack_weight(words, scales, fmt):
    g, _, n = scales.shape
    words = np.ascontiguousarray(words).reshape(g, 128, n, -1)
    if fmt == "e4m3":
        vals = words.view(ml_dtypes.float8_e4m3fn).astype(np.float64)
    else:
        nib = np.empty((g, 128, n, 4), np.uint8)
        nib[..., 0::2] = words & 0xF
        nib[..., 1::2] = words >> 4
        vals = E2M1[nib]
    vals = vals * np.repeat(np.exp2(scales.astype(np.float64) - 127.0), 8, axis=1)[..., None]
    return vals.transpose(0, 1, 3, 2).reshape(g * 512, n)


def gelu(v):
    return 0.5 * v * (1.0 + np.tanh(np.sqrt(2.0 / np.pi) * (v + 0.044715 * v**3)))


K, H, N, T, S, P = 1024, 1024, 512, 4096, 1024, 512

def setup_inputs():
    n = np.random.standard_normal
    s = mx_kscale(K)[:, None]
    u = mx_kscale(H)[:, None]
    tab_words, tab_scales = pack_weight(n((K, T)) * s, "e4m3")
    w1_words, w1_scales = pack_weight(0.8 * n((K, H)) / np.sqrt(K) / s, "e2m1")
    w2 = (n((K, H)) / np.sqrt(K) / s * u.T).astype(np.float32)
    w3 = (n((H, N)) / np.sqrt(H) / u).astype(np.float32)
    w4_words, w4_scales = pack_weight(n((H, N)) / np.sqrt(H) / u, "e4m3")
    return {"tab_words": tab_words, "tab_scales": tab_scales,
            "offs": striped(np.random.permutation(T)[:S]),
            "w1_words": w1_words, "w1_scales": w1_scales, "w2": w2,
            "pos1": striped(np.random.permutation(S)[:P]),
            "pos2": striped(np.random.permutation(S)[:P]),
            "pos3": striped(np.random.permutation(S)[:P]),
            "w3": w3, "w4_words": w4_words, "w4_scales": w4_scales}

def reference(tab_words, tab_scales, offs, w1_words, w1_scales, w2,
              pos1, pos2, pos3, w3, w4_words, w4_scales):
    v = unpack_weight(tab_words, tab_scales, "e4m3")[:, unstriped(offs)]
    buy = unpack_weight(w1_words, w1_scales, "e2m1").T @ v
    link = mxq(f64(w2), 0, "e4m3").T @ v
    buyer = buy[:, unstriped(pos1)]
    device = link[:, unstriped(pos2)]
    address = link[:, unstriped(pos3)]
    z = np.square(buyer) * device - address
    zq = mxq(z, 0, "e4m3")
    y = mxq(f64(w3), 0, "e4m3").T @ zq
    gate = unpack_weight(w4_words, w4_scales, "e4m3").T @ zq
    return y / (1.0 + np.exp(-gate))

@@ -1,0 +1,266 @@
+from contextlib import ExitStack
+
+import concourse.mybir as mybir
+
+K, H, N, T, S, R = 1024, 1024, 512, 4096, 1024, 512
+FLOPS = 2 * (2 * K * H * S + 2 * H * N * R)
+
+F32 = mybir.dt.float32
+BF16 = mybir.dt.bfloat16
+I32 = mybir.dt.int32
+U32 = mybir.dt.uint32
+U16 = mybir.dt.uint16
+U8 = mybir.dt.uint8
+FP8X4 = mybir.dt.float8_e4m3fn_x4
+FP4X4 = mybir.dt.float4_e2m1fn_x4
+ACT = mybir.ActivationFunctionType
+ALU = mybir.AluOpType
+
+P = 128
+BANK = 512
+CHUNKS = ((0, 256), (256, 128), (384, 128))
+WINDOWS = 12
+
+
+def tile_list_refund_ring_links_kernel(
+    tc, tab_words, tab_scales, offs, w1_words, w1_scales, w2, pos1, pos2, pos3, w3, w4_words, w4_scales, out
+):
+    nc = tc.nc
+    with ExitStack() as ctx:
+        lists = ctx.enter_context(tc.tile_pool(name="lists", bufs=1))
+        sb = ctx.enter_context(tc.tile_pool(name="sb", bufs=1))
+        psum = ctx.enter_context(tc.psum_pool(name="psum", bufs=1))
+
+        def tile(shape, dtype, name, tag=None):
+            return sb.tile(shape, dtype, name=name, tag=tag or name, align_bytes=64)
+
+        banks = [psum.tile([P, BANK], F32, name="bank%d" % i) for i in range(8)]
+
+        idx = lists.tile([P, S // 16], U16, name="idx")
+        nc.sync.dma_start(idx[:], offs)
+        ts_rows = tile([P, T], U8, "ts_rows", "table1")
+        nc.sync.dma_start(
+            ts_rows[0:32, :].bitcast(I32), tab_scales.rearrange("a q t -> (a q) t").bitcast(I32)
+        )
+        picks = []
+        for name, src in (("p1", pos1), ("p2", pos2), ("p3", pos3)):
+            pick = lists.tile([P, R // 16], U16, name=name)
+            nc.sync.dma_start(pick[:], src)
+            picks.append(pick)
+        p1, p2, p3 = picks
+        w1_raw = tile([P, 2, 512], U32, "w1_raw", "packed_w")
+        nc.sync.dma_start(w1_raw[:].bitcast(I32), w1_words.rearrange("a p c -> p a c").bitcast(I32))
+
+        def load_table(a):
+            words = tile([P, T], U32, "table%d" % a)
+            nc.sync.dma_start(
+                words[:].bitcast(I32), tab_words[a].rearrange("p t i -> p (t i)").bitcast(I32)
+            )
+            return words
+
+        table = [load_table(0)]
+
+        def load_w2(b, a, dst):
+            rows = w2[512 * a : 512 * a + 512, 512 * b : 512 * b + 512]
+            nc.sync.dma_start(dst, rows.rearrange("(p j) c -> p j c", j=4))
+
+        w1s_raw = tile([P, 2, H], U8, "w1s_raw", "packed_s")
+        nc.vector.memset(w1s_raw[:].rearrange("p a c -> p (a c)").bitcast(I32), 0)
+        for q in range(4):
+            nc.gpsimd.dma_start(
+                w1s_raw[32 * q : 32 * q + 4].bitcast(I32),
+                w1_scales[:, 4 * q : 4 * q + 4, :].rearrange("a r c -> r a c").bitcast(I32),
+            )
+        nc.vector.memset(ts_rows[32:64, :].bitcast(I32), 0)
+        nc.vector.memset(ts_rows[64:128, :].bitcast(I32), 0)
+        v_scale = [tile([P, S], U8, "v_scale%d" % a) for a in range(2)]
+        for a in range(2):
+            nc.vector.memset(v_scale[a][:].bitcast(I32), 0)
+
+        ts_picked = tile([P, S], U8, "ts_picked", "w2_raw0")
+        nc.vector.tensor_copy(ts_picked[:], ts_rows[:].indirect(idx[:]))
+        table.append(load_table(1))
+        for a in range(2):
+            for q in range(4):
+                nc.scalar.dma_start(
+                    v_scale[a][32 * q : 32 * q + 4, :].bitcast(I32),
+                    ts_picked[16 * a + 4 * q : 16 * a + 4 * q + 4, :].bitcast(I32),
+                )
+
+        w2_raw0 = tile([P, 2, 4, 512], F32, "w2_raw0")
+        for a in range(2):
+            load_w2(0, a, w2_raw0[:, a])
+
+        w1_codes = tile([P, 4 * H], U8, "w1_codes")
+        nc.vector.tensor_copy(
+            w1_codes[:].bitcast(U16).rearrange("p (g t m) -> p g t m", t=4, m=P),
+            w1_raw[:].rearrange("p a c -> p (a c)").bitcast(U16).rearrange("p (g m t) -> p g t m", t=4, m=P),
+        )
+        w1_scale = tile([P, 2 * H], U8, "w1_scale")
+        nc.vector.tensor_copy(
+            w1_scale[:].rearrange("p (g t m) -> p g t m", t=4, m=P),
+            w1s_raw[:].rearrange("p a (b m t) -> p (a b) t m", t=4, m=P),
+        )
+
+        v_words = [[tile([P, BANK], U32, "v_words%d%d" % (a, h)) for h in range(2)] for a in range(2)]
+        for a in range(2):
+            for h in range(2):
+                nc.vector.tensor_copy(v_words[a][h][:], table[a][:].indirect(idx[:, 32 * h : 32 * h + 32]))
+
+        w2_raw1 = tile([P, 2, 4, 512], F32, "w2_raw1", "table0")
+        for a in range(2):
+            load_w2(1, a, w2_raw1[:, a])
+        w3_raw = tile([P, 2, 4, N], F32, "w3_raw", "table1")
+        nc.sync.dma_start(w3_raw[:], w3.rearrange("(b p j) n -> p b j n", p=P, j=4))
+
+        windows = [tile([P, S], F32, "window%d" % i) for i in range(WINDOWS)]
+
+        def first_stage(k, lhs, func):
+            window = windows[k % WINDOWS]
+            for h in range(2):
+                bank = banks[(2 * k + h) % 8]
+                for a in range(2):
+                    codes, scale = lhs(a)
+                    nc.tensor.matmul_mx(
+                        bank[:], lhsT=codes, lhsT_scale=scale,
+                        rhs=v_words[a][h][:].bitcast(FP8X4), rhs_scale=v_scale[a][:, BANK * h : BANK * h + BANK],
+                        start=(a == 0), stop=(a == 1),
+                    )
+                nc.scalar.activation(window[:, BANK * h : BANK * h + BANK], bank[:], func)
+            return window
+
+        def quantise(rounded, width, name):
+            codes = tile([P, width], U32, name + "_codes")
+            scale = tile([P, width], U8, name + "_scale")
+            nc.vector.quantize_mx(out=codes[:].bitcast(FP8X4), scales=scale[:], in_=rounded)
+            return codes, scale
+
+        def w2_views(dst, raw):
+            return dst.rearrange("p (t m j) -> p m t j", t=4, j=4), raw.rearrange("p j (m t) -> p m t j", t=4)
+
+        def weave_views(dst, raw):
+            return dst.rearrange("p (c i j) -> p c j i", i=4, j=4), raw.rearrange("p j (c i) -> p c j i", i=4)
+
+        w2q = {}
+        for a in range(2):
+            rounded = tile([P, 2048], BF16, "w2_round0%d" % a)
+            dst, src = w2_views(rounded[:], w2_raw0[:, a])
+            nc.vector.tensor_copy(dst, src)
+            w2q[0, a] = quantise(rounded[:], 512, "w2q0%d" % a)
+
+        w4_codes = tile([P, 2, N], U32, "w4_codes", "w2_raw0")
+        nc.sync.dma_start(w4_codes[:].bitcast(I32), w4_words.rearrange("b p c i -> p b (c i)").bitcast(I32))
+        w4_scale = tile([P, 2, N], U8, "w4_scale", "w2_round00")
+        nc.vector.memset(w4_scale[:].rearrange("p b c -> p (b c)").bitcast(I32), 0)
+        for q in range(4):
+            nc.sync.dma_start(
+                w4_scale[32 * q : 32 * q + 4].bitcast(I32),
+                w4_scales[:, 4 * q : 4 * q + 4, :].rearrange("b r c -> r b c").bitcast(I32),
+            )
+
+        buyer2 = [tile([P, 4, R], F32, "buyer2_%d" % b) for b in range(2)]
+        for s in range(8):
+            def w1_slice(a):
+                c = H * a + P * s
+                return w1_codes[:, 2 * c : 2 * c + 2 * P].bitcast(FP4X4), w1_scale[:, c : c + P]
+
+            window = first_stage(s, w1_slice, ACT.Square)
+            nc.vector.tensor_copy(buyer2[s // 4][:, s % 4, :], window[:].indirect(p1[:]))
+
+        link = {}
+        prod = [tile([P, 4, R], F32, "prod%d" % b) for b in range(2)]
+
+        def link_block(b):
+            for t in range(4):
+                def w2_slice(a):
+                    codes, scale = w2q[b, a]
+                    return codes[:, P * t : P * t + P].bitcast(FP8X4), scale[:, P * t : P * t + P]
+
+                link[b, t] = first_stage(8 + 4 * b + t, w2_slice, ACT.Copy)
+                nc.vector.tensor_tensor(prod[b][:, t, :], link[b, t][:].indirect(p2[:]), buyer2[b][:, t, :], ALU.mult)
+
+        def minus_z(b, m0, width, name, tag):
+            zneg = tile([P, 4, width], F32, name, tag)
+            for t in range(4):
+                nc.vector.tensor_tensor(
+                    zneg[:, t, :],
+                    link[b, t][:].indirect(p3[:, m0 // 16 : (m0 + width) // 16]),
+                    prod[b][:, t, m0 : m0 + width],
+                    ALU.subtract,
+                )
+            return zneg
+
+        link_block(0)
+
+        w2_round1 = tile([P, 2, 2048], BF16, "w2_round1", "stage_a")
+        for a in range(2):
+            dst, src = w2_views(w2_round1[:, a, :], w2_raw1[:, a])
+            nc.scalar.activation(dst, src, ACT.Copy)
+            w2q[1, a] = quantise(w2_round1[:, a, :], 512, "w2q1%d" % a)
+        zneg0 = minus_z(0, 0, R, "zneg0", "stage_a")
+
+        link_block(1)
+
+        w3_round = tile([P, 2, 2048], BF16, "w3_round", "stage_b")
+        w3q = []
+        for b in range(2):
+            dst, src = weave_views(w3_round[:, b, :], w3_raw[:, b])
+            nc.scalar.activation(dst, src, ACT.Copy)
+            w3q.append(quantise(w3_round[:, b, :], N, "w3q%d" % b))
+
+        z0_round = tile([P, 4 * R], BF16, "z0_round", "stage_c")
+        dst, src = weave_views(z0_round[:], zneg0[:])
+        nc.scalar.activation(dst, src, ACT.Copy, scale=-1.0)
+        zq0 = quantise(z0_round[:], R, "zq0")
+
+        def regions(first_bank, width):
+            per_bank = BANK // width
+            return [(banks[first_bank + n // per_bank], (n % per_bank) * width, n % per_bank) for n in range(4)]
+
+        def second_stage(b, zq, z0, width, gate_at, y_at):
+            codes, scale = zq
+            per_bank = BANK // width
+            for places, weight in ((gate_at, 4), (y_at, 3)):
+                for n, (bank, c0, slot) in enumerate(places):
+                    cols = slice(P * n, P * n + P)
+                    if weight == 4:
+                        lhs, lhs_scale = w4_codes[:, b, cols], w4_scale[:, b, cols]
+                    else:
+                        lhs, lhs_scale = w3q[b][0][:, cols], w3q[b][1][:, cols]
+                    nc.tensor.matmul_mx(
+                        bank[:, c0 : c0 + width], lhsT=lhs.bitcast(FP8X4), lhsT_scale=lhs_scale,
+                        rhs=codes[:, z0 : z0 + width].bitcast(FP8X4), rhs_scale=scale[:, z0 : z0 + width],
+                        start=(b == 0 and slot == 0), stop=(b == 1 and slot == per_bank - 1),
+                    )
+
+        places = []
+        first = 0
+        for m0, width in CHUNKS:
+            count = 4 * width // BANK
+            places.append((first, count, regions(first, width), regions(first + count, width)))
+            first += 2 * count
+        for (m0, width), (first, count, gate_at, y_at) in zip(CHUNKS, places):
+            second_stage(0, zq0, m0, width, gate_at, y_at)
+
+        out_view = out.rearrange("(n p) m -> p n m", p=P)
+        zneg_tags = ("stage_b", "stage_c", None)
+        for i, ((m0, width), (first, count, gate_at, y_at)) in enumerate(zip(CHUNKS, places)):
+            zneg = minus_z(1, m0, width, "zneg1%d" % i, zneg_tags[i])
+            rounded = tile([P, 4 * width], BF16, "z1_round%d" % i)
+            dst, src = weave_views(rounded[:], zneg[:])
+            if i < len(CHUNKS) - 1:
+                nc.scalar.activation(dst, src, ACT.Copy, scale=-1.0)
+            else:
+                nc.vector.tensor_scalar_mul(dst, src, -1.0)
+            zq = quantise(rounded[:], width, "zq1%d" % i)
+            second_stage(1, zq, 0, width, gate_at, y_at)
+            per_bank = BANK // width
+            for j in range(count):
+                gate = tile([P, BANK], F32, "gate%d%d" % (i, j))
+                nc.scalar.activation(gate[:], banks[first + j][:], ACT.Sigmoid)
+                res = tile([P, BANK], F32, "res%d%d" % (i, j), "window%d" % (4 + first // 2 + j))
+                nc.vector.tensor_tensor(res[:], banks[first + count + j][:], gate[:], ALU.mult)
+                nc.sync.dma_start(
+                    out_view[:, per_bank * j : per_bank * j + per_bank, m0 : m0 + width],
+                    res[:].rearrange("p (n m) -> p n m", m=width),
+                )

@@ -36,9 +36,12 @@ def tile_list_refund_ring_links_kernel(
 
         banks = [psum.tile([P, BANK], F32, name="bank%d" % i) for i in range(8)]
 
+        warm = tile([P, 2], F32, "warm")
+        nc.vector.memset(warm[:, 0:1], 0.0)
+        nc.scalar.activation(warm[:, 1:2], warm[:, 0:1], ACT.Sigmoid)
         idx = lists.tile([P, S // 16], U16, name="idx")
         nc.sync.dma_start(idx[:], offs)
-        ts_rows = tile([P, T], U8, "ts_rows", "table1")
+        ts_rows = tile([P, T], U8, "ts_rows")
         nc.sync.dma_start(
             ts_rows[0:32, :].bitcast(I32), tab_scales.rearrange("a q t -> (a q) t").bitcast(I32)
         )
@@ -58,7 +61,7 @@ def tile_list_refund_ring_links_kernel(
             )
             return words
 
-        table = [load_table(0)]
+        table = [load_table(a) for a in range(2)]
 
         def load_w2(b, a, dst):
             rows = w2[512 * a : 512 * a + 512, 512 * b : 512 * b + 512]
@@ -79,10 +82,10 @@ def tile_list_refund_ring_links_kernel(
 
         ts_picked = tile([P, S], U8, "ts_picked", "w2_raw0")
         nc.vector.tensor_copy(ts_picked[:], ts_rows[:].indirect(idx[:]))
-        table.append(load_table(1))
         for a in range(2):
             for q in range(4):
-                nc.scalar.dma_start(
+                queue = nc.gpsimd if (a, q) == (1, 3) else nc.scalar
+                queue.dma_start(
                     v_scale[a][32 * q : 32 * q + 4, :].bitcast(I32),
                     ts_picked[16 * a + 4 * q : 16 * a + 4 * q + 4, :].bitcast(I32),
                 )
@@ -142,15 +145,19 @@ def tile_list_refund_ring_links_kernel(
             return dst.rearrange("p (c i j) -> p c j i", i=4, j=4), raw.rearrange("p j (c i) -> p c j i", i=4)
 
         w2q = {}
-        for a in range(2):
-            rounded = tile([P, 2048], BF16, "w2_round0%d" % a)
-            dst, src = w2_views(rounded[:], w2_raw0[:, a])
-            nc.vector.tensor_copy(dst, src)
-            w2q[0, a] = quantise(rounded[:], 512, "w2q0%d" % a)
+        for u in range(2):
+            for a in range(2):
+                rounded = tile([P, 1024], BF16, "w2_round0%d%d" % (u, a))
+                nc.gpsimd.tensor_scalar(
+                    rounded[:].rearrange("p (t m j) -> p m t j", t=2, j=4),
+                    w2_raw0[:, a].rearrange("p j (m t) -> p m t j", t=4)[:, :, 2 * u : 2 * u + 2, :],
+                    1.0, 0.0, ALU.mult, ALU.add,
+                )
+                w2q[0, a, u] = quantise(rounded[:], 256, "w2q0%d%d" % (u, a))
 
         w4_codes = tile([P, 2, N], U32, "w4_codes", "w2_raw0")
         nc.sync.dma_start(w4_codes[:].bitcast(I32), w4_words.rearrange("b p c i -> p b (c i)").bitcast(I32))
-        w4_scale = tile([P, 2, N], U8, "w4_scale", "w2_round00")
+        w4_scale = tile([P, 2, N], U8, "w4_scale", "w2_round000")
         nc.vector.memset(w4_scale[:].rearrange("p b c -> p (b c)").bitcast(I32), 0)
         for q in range(4):
             nc.sync.dma_start(
@@ -173,8 +180,9 @@ def tile_list_refund_ring_links_kernel(
         def link_block(b):
             for t in range(4):
                 def w2_slice(a):
-                    codes, scale = w2q[b, a]
-                    return codes[:, P * t : P * t + P].bitcast(FP8X4), scale[:, P * t : P * t + P]
+                    codes, scale = w2q[b, a, t // 2]
+                    c = P * (t % 2 if b == 0 else t)
+                    return codes[:, c : c + P].bitcast(FP8X4), scale[:, c : c + P]
 
                 link[b, t] = first_stage(8 + 4 * b + t, w2_slice, ACT.Copy)
                 nc.vector.tensor_tensor(prod[b][:, t, :], link[b, t][:].indirect(p2[:]), buyer2[b][:, t, :], ALU.mult)
@@ -196,7 +204,7 @@ def tile_list_refund_ring_links_kernel(
         for a in range(2):
             dst, src = w2_views(w2_round1[:, a, :], w2_raw1[:, a])
             nc.scalar.activation(dst, src, ACT.Copy)
-            w2q[1, a] = quantise(w2_round1[:, a, :], 512, "w2q1%d" % a)
+            w2q[1, a, 0] = w2q[1, a, 1] = quantise(w2_round1[:, a, :], 512, "w2q1%d" % a)
         zneg0 = minus_z(0, 0, R, "zneg0", "stage_a")
 
         link_block(1)
@@ -243,7 +251,7 @@ def tile_list_refund_ring_links_kernel(
             second_stage(0, zq0, m0, width, gate_at, y_at)
 
         out_view = out.rearrange("(n p) m -> p n m", p=P)
-        zneg_tags = ("stage_b", "stage_c", None)
+        zneg_tags = ("stage_b", "stage_c", "z1_round0")
         for i, ((m0, width), (first, count, gate_at, y_at)) in enumerate(zip(CHUNKS, places)):
             zneg = minus_z(1, m0, width, "zneg1%d" % i, zneg_tags[i])
             rounded = tile([P, 4 * width], BF16, "z1_round%d" % i)

@@ -67,6 +67,9 @@ def tile_list_refund_ring_links_kernel(
             rows = w2[512 * a : 512 * a + 512, 512 * b : 512 * b + 512]
             nc.sync.dma_start(dst, rows.rearrange("(p j) c -> p j c", j=4))
 
+        w2_raw00 = tile([P, 4, 512], F32, "w2_raw00")
+        load_w2(0, 0, w2_raw00[:])
+
         w1s_raw = tile([P, 2, H], U8, "w1s_raw", "packed_s")
         nc.vector.memset(w1s_raw[:].rearrange("p a c -> p (a c)").bitcast(I32), 0)
         for q in range(4):
@@ -80,19 +83,15 @@ def tile_list_refund_ring_links_kernel(
         for a in range(2):
             nc.vector.memset(v_scale[a][:].bitcast(I32), 0)
 
-        ts_picked = tile([P, S], U8, "ts_picked", "w2_raw0")
+        ts_picked = tile([P, S], U8, "ts_picked")
         nc.vector.tensor_copy(ts_picked[:], ts_rows[:].indirect(idx[:]))
         for a in range(2):
             for q in range(4):
-                queue = nc.gpsimd if (a, q) == (1, 3) else nc.scalar
+                queue = nc.gpsimd if a == 1 and q >= 2 else nc.scalar
                 queue.dma_start(
                     v_scale[a][32 * q : 32 * q + 4, :].bitcast(I32),
                     ts_picked[16 * a + 4 * q : 16 * a + 4 * q + 4, :].bitcast(I32),
                 )
-
-        w2_raw0 = tile([P, 2, 4, 512], F32, "w2_raw0")
-        for a in range(2):
-            load_w2(0, a, w2_raw0[:, a])
 
         w1_codes = tile([P, 4 * H], U8, "w1_codes")
         nc.vector.tensor_copy(
@@ -110,11 +109,11 @@ def tile_list_refund_ring_links_kernel(
             for h in range(2):
                 nc.vector.tensor_copy(v_words[a][h][:], table[a][:].indirect(idx[:, 32 * h : 32 * h + 32]))
 
-        w2_raw1 = tile([P, 2, 4, 512], F32, "w2_raw1", "table0")
+        w2_raw01 = tile([P, 4, 512], F32, "w2_raw01", "table0")
+        load_w2(0, 1, w2_raw01[:])
+        w2_raw1 = tile([P, 2, 4, 512], F32, "w2_raw1", "table1")
         for a in range(2):
             load_w2(1, a, w2_raw1[:, a])
-        w3_raw = tile([P, 2, 4, N], F32, "w3_raw", "table1")
-        nc.sync.dma_start(w3_raw[:], w3.rearrange("(b p j) n -> p b j n", p=P, j=4))
 
         windows = [tile([P, S], F32, "window%d" % i) for i in range(WINDOWS)]
 
@@ -145,19 +144,17 @@ def tile_list_refund_ring_links_kernel(
             return dst.rearrange("p (c i j) -> p c j i", i=4, j=4), raw.rearrange("p j (c i) -> p c j i", i=4)
 
         w2q = {}
-        for u in range(2):
-            for a in range(2):
-                rounded = tile([P, 1024], BF16, "w2_round0%d%d" % (u, a))
-                nc.gpsimd.tensor_scalar(
-                    rounded[:].rearrange("p (t m j) -> p m t j", t=2, j=4),
-                    w2_raw0[:, a].rearrange("p j (m t) -> p m t j", t=4)[:, :, 2 * u : 2 * u + 2, :],
-                    1.0, 0.0, ALU.mult, ALU.add,
-                )
-                w2q[0, a, u] = quantise(rounded[:], 256, "w2q0%d%d" % (u, a))
+        for a, raw in enumerate((w2_raw00, w2_raw01)):
+            rounded = tile([P, 2048], BF16, "w2_round0%d" % a)
+            dst, src = w2_views(rounded[:], raw[:])
+            nc.vector.tensor_copy(dst, src)
+            w2q[0, a] = quantise(rounded[:], 512, "w2q0%d" % a)
 
-        w4_codes = tile([P, 2, N], U32, "w4_codes", "w2_raw0")
+        w3_raw = tile([P, 2, 4, N], F32, "w3_raw", "table0")
+        nc.sync.dma_start(w3_raw[:], w3.rearrange("(b p j) n -> p b j n", p=P, j=4))
+        w4_codes = tile([P, 2, N], U32, "w4_codes", "w2_raw00")
         nc.sync.dma_start(w4_codes[:].bitcast(I32), w4_words.rearrange("b p c i -> p b (c i)").bitcast(I32))
-        w4_scale = tile([P, 2, N], U8, "w4_scale", "w2_round000")
+        w4_scale = tile([P, 2, N], U8, "w4_scale", "w2_round01")
         nc.vector.memset(w4_scale[:].rearrange("p b c -> p (b c)").bitcast(I32), 0)
         for q in range(4):
             nc.sync.dma_start(
@@ -180,15 +177,13 @@ def tile_list_refund_ring_links_kernel(
         def link_block(b):
             for t in range(4):
                 def w2_slice(a):
-                    codes, scale = w2q[b, a, t // 2]
-                    c = P * (t % 2 if b == 0 else t)
-                    return codes[:, c : c + P].bitcast(FP8X4), scale[:, c : c + P]
+                    codes, scale = w2q[b, a]
+                    return codes[:, P * t : P * t + P].bitcast(FP8X4), scale[:, P * t : P * t + P]
 
                 link[b, t] = first_stage(8 + 4 * b + t, w2_slice, ACT.Copy)
                 nc.vector.tensor_tensor(prod[b][:, t, :], link[b, t][:].indirect(p2[:]), buyer2[b][:, t, :], ALU.mult)
 
-        def minus_z(b, m0, width, name, tag):
-            zneg = tile([P, 4, width], F32, name, tag)
+        def minus_z(b, m0, width, zneg):
             for t in range(4):
                 nc.vector.tensor_tensor(
                     zneg[:, t, :],
@@ -200,12 +195,13 @@ def tile_list_refund_ring_links_kernel(
 
         link_block(0)
 
-        w2_round1 = tile([P, 2, 2048], BF16, "w2_round1", "stage_a")
-        for a in range(2):
-            dst, src = w2_views(w2_round1[:, a, :], w2_raw1[:, a])
+        stage_a = tile([P, 4 * R], F32, "stage_a")
+        w2_round10 = tile([P, 2048], BF16, "w2_round10", "w2_round00")
+        for a, rounded in enumerate((w2_round10[:], stage_a[:, 2 * R : 3 * R + R].bitcast(BF16))):
+            dst, src = w2_views(rounded, w2_raw1[:, a])
             nc.scalar.activation(dst, src, ACT.Copy)
-            w2q[1, a, 0] = w2q[1, a, 1] = quantise(w2_round1[:, a, :], 512, "w2q1%d" % a)
-        zneg0 = minus_z(0, 0, R, "zneg0", "stage_a")
+            w2q[1, a] = quantise(rounded, 512, "w2q1%d" % a)
+        zneg0 = minus_z(0, 0, R, stage_a[:].rearrange("p (t m) -> p t m", t=4))
 
         link_block(1)
 
@@ -217,7 +213,7 @@ def tile_list_refund_ring_links_kernel(
             w3q.append(quantise(w3_round[:, b, :], N, "w3q%d" % b))
 
         z0_round = tile([P, 4 * R], BF16, "z0_round", "stage_c")
-        dst, src = weave_views(z0_round[:], zneg0[:])
+        dst, src = weave_views(z0_round[:], zneg0)
         nc.scalar.activation(dst, src, ACT.Copy, scale=-1.0)
         zq0 = quantise(z0_round[:], R, "zq0")
 
@@ -253,22 +249,24 @@ def tile_list_refund_ring_links_kernel(
         out_view = out.rearrange("(n p) m -> p n m", p=P)
         zneg_tags = ("stage_b", "stage_c", "z1_round0")
         for i, ((m0, width), (first, count, gate_at, y_at)) in enumerate(zip(CHUNKS, places)):
-            zneg = minus_z(1, m0, width, "zneg1%d" % i, zneg_tags[i])
+            zneg = minus_z(1, m0, width, tile([P, 4, width], F32, "zneg1%d" % i, zneg_tags[i])[:])
             rounded = tile([P, 4 * width], BF16, "z1_round%d" % i)
-            dst, src = weave_views(rounded[:], zneg[:])
+            dst, src = weave_views(rounded[:], zneg)
             if i < len(CHUNKS) - 1:
                 nc.scalar.activation(dst, src, ACT.Copy, scale=-1.0)
             else:
                 nc.vector.tensor_scalar_mul(dst, src, -1.0)
             zq = quantise(rounded[:], width, "zq1%d" % i)
             second_stage(1, zq, 0, width, gate_at, y_at)
-            per_bank = BANK // width
-            for j in range(count):
-                gate = tile([P, BANK], F32, "gate%d%d" % (i, j))
-                nc.scalar.activation(gate[:], banks[first + j][:], ACT.Sigmoid)
-                res = tile([P, BANK], F32, "res%d%d" % (i, j), "window%d" % (4 + first // 2 + j))
-                nc.vector.tensor_tensor(res[:], banks[first + count + j][:], gate[:], ALU.mult)
+            for j in range(2):
+                c0 = (2 * j * width) % BANK
+                cols = slice(c0, c0 + 2 * width)
+                k = 2 * j * width // BANK
+                gate = tile([P, 2 * width], F32, "gate%d%d" % (i, j))
+                nc.scalar.activation(gate[:], banks[first + k][:, cols], ACT.Sigmoid)
+                res = tile([P, 2 * width], F32, "res%d%d" % (i, j))
+                nc.vector.tensor_tensor(res[:], banks[first + count + k][:, cols], gate[:], ALU.mult)
                 nc.sync.dma_start(
-                    out_view[:, per_bank * j : per_bank * j + per_bank, m0 : m0 + width],
+                    out_view[:, 2 * j : 2 * j + 2, m0 : m0 + width],
                     res[:].rearrange("p (n m) -> p n m", m=width),
                 )

@@ -39,6 +39,10 @@ def tile_list_refund_ring_links_kernel(
         warm = tile([P, 2], F32, "warm")
         nc.vector.memset(warm[:, 0:1], 0.0)
         nc.scalar.activation(warm[:, 1:2], warm[:, 0:1], ACT.Sigmoid)
+        w1s_rows = tile([P, H], U8, "w1s_rows")
+        nc.sync.dma_start(
+            w1s_rows[0:32, :].bitcast(I32), w1_scales.rearrange("a q c -> (a q) c").bitcast(I32)
+        )
         idx = lists.tile([P, S // 16], U16, name="idx")
         nc.sync.dma_start(idx[:], offs)
         ts_rows = tile([P, T], U8, "ts_rows")
@@ -51,7 +55,7 @@ def tile_list_refund_ring_links_kernel(
             nc.sync.dma_start(pick[:], src)
             picks.append(pick)
         p1, p2, p3 = picks
-        w1_raw = tile([P, 2, 512], U32, "w1_raw", "packed_w")
+        w1_raw = tile([P, 2, 512], U32, "w1_raw")
         nc.sync.dma_start(w1_raw[:].bitcast(I32), w1_words.rearrange("a p c -> p a c").bitcast(I32))
 
         def load_table(a):
@@ -61,47 +65,42 @@ def tile_list_refund_ring_links_kernel(
             )
             return words
 
-        table = [load_table(a) for a in range(2)]
-
         def load_w2(b, a, dst):
             rows = w2[512 * a : 512 * a + 512, 512 * b : 512 * b + 512]
             nc.sync.dma_start(dst, rows.rearrange("(p j) c -> p j c", j=4))
 
+        table = [load_table(0)]
         w2_raw00 = tile([P, 4, 512], F32, "w2_raw00")
         load_w2(0, 0, w2_raw00[:])
 
-        w1s_raw = tile([P, 2, H], U8, "w1s_raw", "packed_s")
-        nc.vector.memset(w1s_raw[:].rearrange("p a c -> p (a c)").bitcast(I32), 0)
-        for q in range(4):
-            nc.gpsimd.dma_start(
-                w1s_raw[32 * q : 32 * q + 4].bitcast(I32),
-                w1_scales[:, 4 * q : 4 * q + 4, :].rearrange("a r c -> r a c").bitcast(I32),
-            )
-        nc.vector.memset(ts_rows[32:64, :].bitcast(I32), 0)
-        nc.vector.memset(ts_rows[64:128, :].bitcast(I32), 0)
-        v_scale = [tile([P, S], U8, "v_scale%d" % a) for a in range(2)]
+        for rows in (w1s_rows, ts_rows):
+            nc.vector.memset(rows[32:64, :].bitcast(I32), 0)
+            nc.vector.memset(rows[64:128, :].bitcast(I32), 0)
+        planes = [tile([P, S + H], U8, "planes%d" % a) for a in range(2)]
         for a in range(2):
-            nc.vector.memset(v_scale[a][:].bitcast(I32), 0)
+            nc.vector.memset(planes[a][:].bitcast(I32), 0)
 
-        ts_picked = tile([P, S], U8, "ts_picked")
+        scale_rows = tile([P, S + H], U8, "scale_rows", "w4_codes")
+        nc.vector.tensor_copy(
+            scale_rows[:, S : S + H].rearrange("p (b t m) -> p b t m", t=4, m=P),
+            w1s_rows[:].rearrange("p (b m t) -> p b t m", t=4, m=P),
+        )
+        ts_picked = tile([P, S], U8, "ts_picked", "table1")
         nc.vector.tensor_copy(ts_picked[:], ts_rows[:].indirect(idx[:]))
+        nc.vector.tensor_copy(scale_rows[:, 0:S].bitcast(I32), ts_picked[:].bitcast(I32))
         for a in range(2):
             for q in range(4):
-                queue = nc.gpsimd if a == 1 and q >= 2 else nc.scalar
-                queue.dma_start(
-                    v_scale[a][32 * q : 32 * q + 4, :].bitcast(I32),
-                    ts_picked[16 * a + 4 * q : 16 * a + 4 * q + 4, :].bitcast(I32),
+                nc.sync.dma_start(
+                    planes[a][32 * q : 32 * q + 4, :].bitcast(I32),
+                    scale_rows[16 * a + 4 * q : 16 * a + 4 * q + 4, :].bitcast(I32),
                 )
+            if a == 0:
+                table.append(load_table(1))
 
         w1_codes = tile([P, 4 * H], U8, "w1_codes")
         nc.vector.tensor_copy(
             w1_codes[:].bitcast(U16).rearrange("p (g t m) -> p g t m", t=4, m=P),
             w1_raw[:].rearrange("p a c -> p (a c)").bitcast(U16).rearrange("p (g m t) -> p g t m", t=4, m=P),
-        )
-        w1_scale = tile([P, 2 * H], U8, "w1_scale")
-        nc.vector.tensor_copy(
-            w1_scale[:].rearrange("p (g t m) -> p g t m", t=4, m=P),
-            w1s_raw[:].rearrange("p a (b m t) -> p (a b) t m", t=4, m=P),
         )
 
         v_words = [[tile([P, BANK], U32, "v_words%d%d" % (a, h)) for h in range(2)] for a in range(2)]
@@ -115,17 +114,15 @@ def tile_list_refund_ring_links_kernel(
         for a in range(2):
             load_w2(1, a, w2_raw1[:, a])
 
-        windows = [tile([P, S], F32, "window%d" % i) for i in range(WINDOWS)]
-
         def first_stage(k, lhs, func):
-            window = windows[k % WINDOWS]
+            window = tile([P, S], F32, "window_of%d" % k, "window%d" % (k % WINDOWS))
             for h in range(2):
                 bank = banks[(2 * k + h) % 8]
                 for a in range(2):
                     codes, scale = lhs(a)
                     nc.tensor.matmul_mx(
                         bank[:], lhsT=codes, lhsT_scale=scale,
-                        rhs=v_words[a][h][:].bitcast(FP8X4), rhs_scale=v_scale[a][:, BANK * h : BANK * h + BANK],
+                        rhs=v_words[a][h][:].bitcast(FP8X4), rhs_scale=planes[a][:, BANK * h : BANK * h + BANK],
                         start=(a == 0), stop=(a == 1),
                     )
                 nc.scalar.activation(window[:, BANK * h : BANK * h + BANK], bank[:], func)
@@ -144,17 +141,29 @@ def tile_list_refund_ring_links_kernel(
             return dst.rearrange("p (c i j) -> p c j i", i=4, j=4), raw.rearrange("p j (c i) -> p c j i", i=4)
 
         w2q = {}
-        for a, raw in enumerate((w2_raw00, w2_raw01)):
-            rounded = tile([P, 2048], BF16, "w2_round0%d" % a)
+
+        def round_w2_on_vector(a, raw, tag):
+            rounded = tile([P, 2048], BF16, "w2_round0%d" % a, tag)
             dst, src = w2_views(rounded[:], raw[:])
             nc.vector.tensor_copy(dst, src)
             w2q[0, a] = quantise(rounded[:], 512, "w2q0%d" % a)
 
-        w3_raw = tile([P, 2, 4, N], F32, "w3_raw", "table0")
+        round_w2_on_vector(0, w2_raw00, "w2_round10")
+        round_w2_on_vector(1, w2_raw01, "w2_round01")
+        buyer2 = [tile([P, 4, R], F32, "buyer2_0", "table0"), tile([P, 4, R], F32, "buyer2_1")]
+        for s in range(8):
+            def w1_slice(a):
+                c = H * a + P * s
+                return w1_codes[:, 2 * c : 2 * c + 2 * P].bitcast(FP4X4), planes[a][:, S + P * s : S + P * s + P]
+
+            window = first_stage(s, w1_slice, ACT.Square)
+            nc.vector.tensor_copy(buyer2[s // 4][:, s % 4, :], window[:].indirect(p1[:]))
+
+        w3_raw = tile([P, 2, 4, N], F32, "w3_raw", "w2_raw00")
         nc.sync.dma_start(w3_raw[:], w3.rearrange("(b p j) n -> p b j n", p=P, j=4))
-        w4_codes = tile([P, 2, N], U32, "w4_codes", "w2_raw00")
+        w4_codes = tile([P, 2, N], U32, "w4_codes")
         nc.sync.dma_start(w4_codes[:].bitcast(I32), w4_words.rearrange("b p c i -> p b (c i)").bitcast(I32))
-        w4_scale = tile([P, 2, N], U8, "w4_scale", "w2_round01")
+        w4_scale = tile([P, 2, N], U8, "w4_scale", "window5")
         nc.vector.memset(w4_scale[:].rearrange("p b c -> p (b c)").bitcast(I32), 0)
         for q in range(4):
             nc.sync.dma_start(
@@ -162,14 +171,6 @@ def tile_list_refund_ring_links_kernel(
                 w4_scales[:, 4 * q : 4 * q + 4, :].rearrange("b r c -> r b c").bitcast(I32),
             )
 
-        buyer2 = [tile([P, 4, R], F32, "buyer2_%d" % b) for b in range(2)]
-        for s in range(8):
-            def w1_slice(a):
-                c = H * a + P * s
-                return w1_codes[:, 2 * c : 2 * c + 2 * P].bitcast(FP4X4), w1_scale[:, c : c + P]
-
-            window = first_stage(s, w1_slice, ACT.Square)
-            nc.vector.tensor_copy(buyer2[s // 4][:, s % 4, :], window[:].indirect(p1[:]))
 
         link = {}
         prod = [tile([P, 4, R], F32, "prod%d" % b) for b in range(2)]
@@ -196,7 +197,7 @@ def tile_list_refund_ring_links_kernel(
         link_block(0)
 
         stage_a = tile([P, 4 * R], F32, "stage_a")
-        w2_round10 = tile([P, 2048], BF16, "w2_round10", "w2_round00")
+        w2_round10 = tile([P, 2048], BF16, "w2_round10")
         for a, rounded in enumerate((w2_round10[:], stage_a[:, 2 * R : 3 * R + R].bitcast(BF16))):
             dst, src = w2_views(rounded, w2_raw1[:, a])
             nc.scalar.activation(dst, src, ACT.Copy)

@@ -19,7 +19,6 @@ ALU = mybir.AluOpType
 P = 128
 BANK = 512
 CHUNKS = ((0, 256), (256, 128), (384, 128))
-WINDOWS = 12
 
 
 def tile_list_refund_ring_links_kernel(
@@ -36,27 +35,10 @@ def tile_list_refund_ring_links_kernel(
 
         banks = [psum.tile([P, BANK], F32, name="bank%d" % i) for i in range(8)]
 
-        warm = tile([P, 2], F32, "warm")
-        nc.vector.memset(warm[:, 0:1], 0.0)
-        nc.scalar.activation(warm[:, 1:2], warm[:, 0:1], ACT.Sigmoid)
-        w1s_rows = tile([P, H], U8, "w1s_rows")
-        nc.sync.dma_start(
-            w1s_rows[0:32, :].bitcast(I32), w1_scales.rearrange("a q c -> (a q) c").bitcast(I32)
-        )
-        idx = lists.tile([P, S // 16], U16, name="idx")
-        nc.sync.dma_start(idx[:], offs)
-        ts_rows = tile([P, T], U8, "ts_rows")
-        nc.sync.dma_start(
-            ts_rows[0:32, :].bitcast(I32), tab_scales.rearrange("a q t -> (a q) t").bitcast(I32)
-        )
-        picks = []
-        for name, src in (("p1", pos1), ("p2", pos2), ("p3", pos3)):
-            pick = lists.tile([P, R // 16], U16, name=name)
-            nc.sync.dma_start(pick[:], src)
-            picks.append(pick)
-        p1, p2, p3 = picks
-        w1_raw = tile([P, 2, 512], U32, "w1_raw")
-        nc.sync.dma_start(w1_raw[:].bitcast(I32), w1_words.rearrange("a p c -> p a c").bitcast(I32))
+        def load_list(name, src, entries):
+            offsets = lists.tile([P, entries // 16], U16, name=name)
+            nc.sync.dma_start(offsets[:], src)
+            return offsets
 
         def load_table(a):
             words = tile([P, T], U32, "table%d" % a)
@@ -69,53 +51,74 @@ def tile_list_refund_ring_links_kernel(
             rows = w2[512 * a : 512 * a + 512, 512 * b : 512 * b + 512]
             nc.sync.dma_start(dst, rows.rearrange("(p j) c -> p j c", j=4))
 
+        idx = load_list("idx", offs, S)
+        ts_rows = tile([P, T], U8, "ts_rows")
+        nc.sync.dma_start(
+            ts_rows[0:32, :].bitcast(I32), tab_scales.rearrange("a q t -> (a q) t").bitcast(I32)
+        )
+        w1s_rows = tile([P, H], U8, "w1s_rows")
+        nc.sync.dma_start(
+            w1s_rows[0:32, :].bitcast(I32), w1_scales.rearrange("a q c -> (a q) c").bitcast(I32)
+        )
         table = [load_table(0)]
-        w2_raw00 = tile([P, 4, 512], F32, "w2_raw00")
-        load_w2(0, 0, w2_raw00[:])
+        w1_raw = tile([P, 2, 512], U32, "w1_raw")
+        nc.sync.dma_start(w1_raw[:].bitcast(I32), w1_words.rearrange("a p c -> p a c").bitcast(I32))
+        p1 = load_list("p1", pos1, R)
+        p2 = load_list("p2", pos2, R)
+        p3 = load_list("p3", pos3, R)
+        table.append(load_table(1))
 
-        for rows in (w1s_rows, ts_rows):
+        for rows in (ts_rows, w1s_rows):
             nc.vector.memset(rows[32:64, :].bitcast(I32), 0)
             nc.vector.memset(rows[64:128, :].bitcast(I32), 0)
         planes = [tile([P, S + H], U8, "planes%d" % a) for a in range(2)]
-        for a in range(2):
-            nc.vector.memset(planes[a][:].bitcast(I32), 0)
+        nc.vector.memset(planes[1][:].bitcast(I32), 0)
 
-        scale_rows = tile([P, S + H], U8, "scale_rows", "w4_codes")
+        scale_rows = planes[0]
         nc.vector.tensor_copy(
             scale_rows[:, S : S + H].rearrange("p (b t m) -> p b t m", t=4, m=P),
             w1s_rows[:].rearrange("p (b m t) -> p b t m", t=4, m=P),
         )
-        ts_picked = tile([P, S], U8, "ts_picked", "table1")
+        ts_picked = tile([P, S], U8, "ts_picked")
         nc.vector.tensor_copy(ts_picked[:], ts_rows[:].indirect(idx[:]))
         nc.vector.tensor_copy(scale_rows[:, 0:S].bitcast(I32), ts_picked[:].bitcast(I32))
-        for a in range(2):
-            for q in range(4):
-                nc.sync.dma_start(
-                    planes[a][32 * q : 32 * q + 4, :].bitcast(I32),
-                    scale_rows[16 * a + 4 * q : 16 * a + 4 * q + 4, :].bitcast(I32),
-                )
-            if a == 0:
-                table.append(load_table(1))
+        for a, q, queue in (
+            (0, 1, nc.gpsimd), (0, 2, nc.scalar), (0, 3, nc.scalar),
+            (1, 0, nc.sync), (1, 1, nc.sync), (1, 2, nc.sync), (1, 3, nc.sync),
+        ):
+            queue.dma_start(
+                planes[a][32 * q : 32 * q + 4, :].bitcast(I32),
+                scale_rows[16 * a + 4 * q : 16 * a + 4 * q + 4, :].bitcast(I32),
+            )
 
+        v_words = [[tile([P, BANK], U32, "v_words%d%d" % (a, h)) for h in range(2)] for a in range(2)]
+
+        def pick_words(a):
+            for h in range(2):
+                nc.vector.tensor_copy(v_words[a][h][:], table[a][:].indirect(idx[:, 32 * h : 32 * h + 32]))
+
+        pick_words(0)
         w1_codes = tile([P, 4 * H], U8, "w1_codes")
         nc.vector.tensor_copy(
             w1_codes[:].bitcast(U16).rearrange("p (g t m) -> p g t m", t=4, m=P),
             w1_raw[:].rearrange("p a c -> p (a c)").bitcast(U16).rearrange("p (g m t) -> p g t m", t=4, m=P),
         )
+        pick_words(1)
 
-        v_words = [[tile([P, BANK], U32, "v_words%d%d" % (a, h)) for h in range(2)] for a in range(2)]
-        for a in range(2):
-            for h in range(2):
-                nc.vector.tensor_copy(v_words[a][h][:], table[a][:].indirect(idx[:, 32 * h : 32 * h + 32]))
-
-        w2_raw01 = tile([P, 4, 512], F32, "w2_raw01", "table0")
-        load_w2(0, 1, w2_raw01[:])
+        w2_raw = {(0, 0): tile([P, 4, 512], F32, "w2_raw00", "table0"), (0, 1): tile([P, 4, 512], F32, "w2_raw01", "w1_raw")}
+        load_w2(0, 0, w2_raw[0, 0][:])
+        load_w2(0, 1, w2_raw[0, 1][:])
         w2_raw1 = tile([P, 2, 4, 512], F32, "w2_raw1", "table1")
         for a in range(2):
+            w2_raw[1, a] = w2_raw1[:, a]
             load_w2(1, a, w2_raw1[:, a])
 
-        def first_stage(k, lhs, func):
-            window = tile([P, S], F32, "window_of%d" % k, "window%d" % (k % WINDOWS))
+        made = []
+
+        def first_stage(lhs, func):
+            k = len(made)
+            window = tile([P, S], F32, "window%d" % k)
+            made.append(window)
             for h in range(2):
                 bank = banks[(2 * k + h) % 8]
                 for a in range(2):
@@ -134,36 +137,60 @@ def tile_list_refund_ring_links_kernel(
             nc.vector.quantize_mx(out=codes[:].bitcast(FP8X4), scales=scale[:], in_=rounded)
             return codes, scale
 
-        def w2_views(dst, raw):
-            return dst.rearrange("p (t m j) -> p m t j", t=4, j=4), raw.rearrange("p j (m t) -> p m t j", t=4)
-
         def weave_views(dst, raw):
             return dst.rearrange("p (c i j) -> p c j i", i=4, j=4), raw.rearrange("p j (c i) -> p c j i", i=4)
 
         w2q = {}
 
-        def round_w2_on_vector(a, raw, tag):
-            rounded = tile([P, 2048], BF16, "w2_round0%d" % a, tag)
-            dst, src = w2_views(rounded[:], raw[:])
-            nc.vector.tensor_copy(dst, src)
-            w2q[0, a] = quantise(rounded[:], 512, "w2q0%d" % a)
+        def round_w2(b, a, on_vector):
+            rounded = tile([P, 2048], BF16, "w2_round%d%d" % (b, a), "w2_round%d" % a)
+            dst = rounded[:].rearrange("p (t m j) -> p m j t", t=4, j=4)
+            src = w2_raw[b, a][:].rearrange("p j (m t) -> p m j t", t=4)
+            if on_vector:
+                nc.vector.tensor_copy(dst, src)
+            else:
+                nc.scalar.activation(dst, src, ACT.Copy)
+            w2q[b, a] = quantise(rounded[:], 512, "w2q%d%d" % (b, a))
 
-        round_w2_on_vector(0, w2_raw00, "w2_round10")
-        round_w2_on_vector(1, w2_raw01, "w2_round01")
-        buyer2 = [tile([P, 4, R], F32, "buyer2_0", "table0"), tile([P, 4, R], F32, "buyer2_1")]
-        for s in range(8):
+        buyer2 = {}
+        link = {}
+        zneg0 = tile([P, 4, R], F32, "zneg0")
+        prod = [tile([P, 4, R], F32, "prod%d" % b) for b in range(2)]
+
+        def buy_slice(s, dst):
             def w1_slice(a):
                 c = H * a + P * s
                 return w1_codes[:, 2 * c : 2 * c + 2 * P].bitcast(FP4X4), planes[a][:, S + P * s : S + P * s + P]
 
-            window = first_stage(s, w1_slice, ACT.Square)
-            nc.vector.tensor_copy(buyer2[s // 4][:, s % 4, :], window[:].indirect(p1[:]))
+            window = first_stage(w1_slice, ACT.Square)
+            nc.vector.tensor_copy(dst, window[:].indirect(p1[:]))
+            buyer2[s] = dst
 
-        w3_raw = tile([P, 2, 4, N], F32, "w3_raw", "w2_raw00")
+        def link_slice(b, t):
+            def w2_slice(a):
+                codes, scale = w2q[b, a]
+                return codes[:, P * t : P * t + P].bitcast(FP8X4), scale[:, P * t : P * t + P]
+
+            link[b, t] = first_stage(w2_slice, ACT.Copy)
+            nc.vector.tensor_tensor(prod[b][:, t, :], link[b, t][:].indirect(p2[:]), buyer2[4 * b + t], ALU.mult)
+
+        def minus_z(b, t, m0, width, dst):
+            nc.vector.tensor_tensor(
+                dst, link[b, t][:].indirect(p3[:, m0 // 16 : (m0 + width) // 16]),
+                prod[b][:, t, m0 : m0 + width], ALU.subtract,
+            )
+
+        round_w2(0, 0, True)
+        buyer2_0 = tile([P, 4, R], F32, "buyer2_0", "table0")
+        buyer2_1 = tile([P, 4, R], F32, "buyer2_1")
+        for s in range(3):
+            buy_slice(s, buyer2_0[:, s, :])
+        round_w2(0, 1, False)
+        buy_slice(3, buyer2_0[:, 3, :])
+
+        w3_raw = tile([P, 2, 4, N], F32, "w3_raw", "w1_raw")
         nc.sync.dma_start(w3_raw[:], w3.rearrange("(b p j) n -> p b j n", p=P, j=4))
-        w4_codes = tile([P, 2, N], U32, "w4_codes")
-        nc.sync.dma_start(w4_codes[:].bitcast(I32), w4_words.rearrange("b p c i -> p b (c i)").bitcast(I32))
-        w4_scale = tile([P, 2, N], U8, "w4_scale", "window5")
+        w4_scale = tile([P, 2, N], U8, "w4_scale", "window1")
         nc.vector.memset(w4_scale[:].rearrange("p b c -> p (b c)").bitcast(I32), 0)
         for q in range(4):
             nc.sync.dma_start(
@@ -171,40 +198,16 @@ def tile_list_refund_ring_links_kernel(
                 w4_scales[:, 4 * q : 4 * q + 4, :].rearrange("b r c -> r b c").bitcast(I32),
             )
 
-
-        link = {}
-        prod = [tile([P, 4, R], F32, "prod%d" % b) for b in range(2)]
-
-        def link_block(b):
-            for t in range(4):
-                def w2_slice(a):
-                    codes, scale = w2q[b, a]
-                    return codes[:, P * t : P * t + P].bitcast(FP8X4), scale[:, P * t : P * t + P]
-
-                link[b, t] = first_stage(8 + 4 * b + t, w2_slice, ACT.Copy)
-                nc.vector.tensor_tensor(prod[b][:, t, :], link[b, t][:].indirect(p2[:]), buyer2[b][:, t, :], ALU.mult)
-
-        def minus_z(b, m0, width, zneg):
-            for t in range(4):
-                nc.vector.tensor_tensor(
-                    zneg[:, t, :],
-                    link[b, t][:].indirect(p3[:, m0 // 16 : (m0 + width) // 16]),
-                    prod[b][:, t, m0 : m0 + width],
-                    ALU.subtract,
-                )
-            return zneg
-
-        link_block(0)
-
-        stage_a = tile([P, 4 * R], F32, "stage_a")
-        w2_round10 = tile([P, 2048], BF16, "w2_round10")
-        for a, rounded in enumerate((w2_round10[:], stage_a[:, 2 * R : 3 * R + R].bitcast(BF16))):
-            dst, src = w2_views(rounded, w2_raw1[:, a])
-            nc.scalar.activation(dst, src, ACT.Copy)
-            w2q[1, a] = quantise(rounded, 512, "w2q1%d" % a)
-        zneg0 = minus_z(0, 0, R, stage_a[:].rearrange("p (t m) -> p t m", t=4))
-
-        link_block(1)
+        for t in range(4):
+            link_slice(0, t)
+            minus_z(0, t, 0, R, zneg0[:, t, :])
+            if t in (1, 2):
+                round_w2(1, t - 1, False)
+            buy_slice(4 + t, buyer2_1[:, t, :])
+        w4_codes = tile([P, 2, N], U32, "w4_codes", "window5")
+        nc.sync.dma_start(w4_codes[:].bitcast(I32), w4_words.rearrange("b p c i -> p b (c i)").bitcast(I32))
+        for t in range(4):
+            link_slice(1, t)
 
         w3_round = tile([P, 2, 2048], BF16, "w3_round", "stage_b")
         w3q = []
@@ -214,8 +217,8 @@ def tile_list_refund_ring_links_kernel(
             w3q.append(quantise(w3_round[:, b, :], N, "w3q%d" % b))
 
         z0_round = tile([P, 4 * R], BF16, "z0_round", "stage_c")
-        dst, src = weave_views(z0_round[:], zneg0)
-        nc.scalar.activation(dst, src, ACT.Copy, scale=-1.0)
+        dst, src = weave_views(z0_round[:], zneg0[:])
+        nc.scalar.activation(dst, src, ACT.Copy, scale=-0.5)
         zq0 = quantise(z0_round[:], R, "zq0")
 
         def regions(first_bank, width):
@@ -250,13 +253,15 @@ def tile_list_refund_ring_links_kernel(
         out_view = out.rearrange("(n p) m -> p n m", p=P)
         zneg_tags = ("stage_b", "stage_c", "z1_round0")
         for i, ((m0, width), (first, count, gate_at, y_at)) in enumerate(zip(CHUNKS, places)):
-            zneg = minus_z(1, m0, width, tile([P, 4, width], F32, "zneg1%d" % i, zneg_tags[i])[:])
+            zneg = tile([P, 4, width], F32, "zneg1%d" % i, zneg_tags[i])
+            for t in range(4):
+                minus_z(1, t, m0, width, zneg[:, t, :])
             rounded = tile([P, 4 * width], BF16, "z1_round%d" % i)
-            dst, src = weave_views(rounded[:], zneg)
+            dst, src = weave_views(rounded[:], zneg[:])
             if i < len(CHUNKS) - 1:
-                nc.scalar.activation(dst, src, ACT.Copy, scale=-1.0)
+                nc.scalar.activation(dst, src, ACT.Copy, scale=-0.5)
             else:
-                nc.vector.tensor_scalar_mul(dst, src, -1.0)
+                nc.vector.tensor_scalar_mul(dst, src, -0.5)
             zq = quantise(rounded[:], width, "zq1%d" % i)
             second_stage(1, zq, 0, width, gate_at, y_at)
             for j in range(2):
@@ -264,9 +269,11 @@ def tile_list_refund_ring_links_kernel(
                 cols = slice(c0, c0 + 2 * width)
                 k = 2 * j * width // BANK
                 gate = tile([P, 2 * width], F32, "gate%d%d" % (i, j))
-                nc.scalar.activation(gate[:], banks[first + k][:, cols], ACT.Sigmoid)
+                nc.scalar.activation(gate[:], banks[first + k][:, cols], ACT.Tanh)
                 res = tile([P, 2 * width], F32, "res%d%d" % (i, j))
-                nc.vector.tensor_tensor(res[:], banks[first + count + k][:, cols], gate[:], ALU.mult)
+                nc.vector.scalar_tensor_tensor(
+                    res[:], gate[:], 1.0, banks[first + count + k][:, cols], ALU.add, ALU.mult
+                )
                 nc.sync.dma_start(
                     out_view[:, 2 * j : 2 * j + 2, m0 : m0 + width],
                     res[:].rearrange("p (n m) -> p n m", m=width),

@@ -115,21 +115,23 @@ def tile_list_refund_ring_links_kernel(
 
         made = []
 
-        def first_stage(lhs, func):
-            k = len(made)
-            window = tile([P, S], F32, "window%d" % k)
-            made.append(window)
+        def first_stage(*jobs):
+            windows = []
+            for job in jobs:
+                windows.append(tile([P, S], F32, "window%d" % len(made)))
+                made.append(windows[-1])
             for h in range(2):
-                bank = banks[(2 * k + h) % 8]
-                for a in range(2):
-                    codes, scale = lhs(a)
-                    nc.tensor.matmul_mx(
-                        bank[:], lhsT=codes, lhsT_scale=scale,
-                        rhs=v_words[a][h][:].bitcast(FP8X4), rhs_scale=planes[a][:, BANK * h : BANK * h + BANK],
-                        start=(a == 0), stop=(a == 1),
-                    )
-                nc.scalar.activation(window[:, BANK * h : BANK * h + BANK], bank[:], func)
-            return window
+                for i, (lhs, func) in enumerate(jobs):
+                    bank = banks[(2 * (len(made) - len(jobs)) + len(jobs) * h + i) % 8]
+                    for a in range(2):
+                        codes, scale = lhs(a)
+                        nc.tensor.matmul_mx(
+                            bank[:], lhsT=codes, lhsT_scale=scale,
+                            rhs=v_words[a][h][:].bitcast(FP8X4), rhs_scale=planes[a][:, BANK * h : BANK * h + BANK],
+                            start=(a == 0), stop=(a == 1),
+                        )
+                    nc.scalar.activation(windows[i][:, BANK * h : BANK * h + BANK], bank[:], func)
+            return windows
 
         def quantise(rounded, width, name):
             codes = tile([P, width], U32, name + "_codes")
@@ -142,37 +144,53 @@ def tile_list_refund_ring_links_kernel(
 
         w2q = {}
 
-        def round_w2(b, a, on_vector):
-            rounded = tile([P, 2048], BF16, "w2_round%d%d" % (b, a), "w2_round%d" % a)
-            dst = rounded[:].rearrange("p (t m j) -> p m j t", t=4, j=4)
-            src = w2_raw[b, a][:].rearrange("p j (m t) -> p m j t", t=4)
-            if on_vector:
-                nc.vector.tensor_copy(dst, src)
-            else:
-                nc.scalar.activation(dst, src, ACT.Copy)
-            w2q[b, a] = quantise(rounded[:], 512, "w2q%d%d" % (b, a))
+        def round_w2(b):
+            rounded = tile([P, 2, 2048], BF16, "w2_round%d" % b, "w2_round")
+            for a in range(2):
+                dst = rounded[:, a].rearrange("p (t m j) -> p m j t", t=4, j=4)
+                src = w2_raw[b, a][:].rearrange("p j (m t) -> p m j t", t=4)
+                if b == 0:
+                    nc.gpsimd.tensor_scalar(
+                        dst.rearrange("p m j t -> p m t j"), src.rearrange("p m j t -> p m t j"),
+                        1.0, 0.0, ALU.mult, ALU.add,
+                    )
+                else:
+                    nc.scalar.activation(dst, src, ACT.Copy)
+            w2q[b] = quantise(rounded[:].rearrange("p a c -> p (a c)"), 1024, "w2q%d" % b)
 
         buyer2 = {}
         link = {}
         zneg0 = tile([P, 4, R], F32, "zneg0")
         prod = [tile([P, 4, R], F32, "prod%d" % b) for b in range(2)]
 
-        def buy_slice(s, dst):
+        def buy_job(s):
             def w1_slice(a):
                 c = H * a + P * s
                 return w1_codes[:, 2 * c : 2 * c + 2 * P].bitcast(FP4X4), planes[a][:, S + P * s : S + P * s + P]
 
-            window = first_stage(w1_slice, ACT.Square)
+            return w1_slice, ACT.Square
+
+        def link_job(b, t):
+            def w2_slice(a):
+                codes, scale = w2q[b]
+                cols = slice(512 * a + P * t, 512 * a + P * t + P)
+                return codes[:, cols].bitcast(FP8X4), scale[:, cols]
+
+            return w2_slice, ACT.Copy
+
+        def pick_buyer(s, window, dst):
             nc.vector.tensor_copy(dst, window[:].indirect(p1[:]))
             buyer2[s] = dst
 
-        def link_slice(b, t):
-            def w2_slice(a):
-                codes, scale = w2q[b, a]
-                return codes[:, P * t : P * t + P].bitcast(FP8X4), scale[:, P * t : P * t + P]
-
-            link[b, t] = first_stage(w2_slice, ACT.Copy)
+        def pick_device(b, t):
             nc.vector.tensor_tensor(prod[b][:, t, :], link[b, t][:].indirect(p2[:]), buyer2[4 * b + t], ALU.mult)
+
+        def buy_slice(s, dst):
+            pick_buyer(s, first_stage(buy_job(s))[0], dst)
+
+        def link_slice(b, t):
+            link[b, t] = first_stage(link_job(b, t))[0]
+            pick_device(b, t)
 
         def minus_z(b, t, m0, width, dst):
             nc.vector.tensor_tensor(
@@ -180,46 +198,48 @@ def tile_list_refund_ring_links_kernel(
                 prod[b][:, t, m0 : m0 + width], ALU.subtract,
             )
 
-        round_w2(0, 0, True)
-        buyer2_0 = tile([P, 4, R], F32, "buyer2_0", "table0")
-        buyer2_1 = tile([P, 4, R], F32, "buyer2_1")
-        for s in range(3):
-            buy_slice(s, buyer2_0[:, s, :])
-        round_w2(0, 1, False)
-        buy_slice(3, buyer2_0[:, 3, :])
+        buyer2_all = tile([P, 8, R], F32, "buyer2_all")
+        round_w2(0)
+        for s in range(8):
+            buy_slice(s, buyer2_all[:, s, :])
 
-        w3_raw = tile([P, 2, 4, N], F32, "w3_raw", "w1_raw")
-        nc.sync.dma_start(w3_raw[:], w3.rearrange("(b p j) n -> p b j n", p=P, j=4))
-        w4_scale = tile([P, 2, N], U8, "w4_scale", "window1")
-        nc.vector.memset(w4_scale[:].rearrange("p b c -> p (b c)").bitcast(I32), 0)
+        w3_raw = [tile([P, 4, N], F32, "w3_raw%d" % b, tag) for b, tag in enumerate(("table0", "w1_raw"))]
+        for b in range(2):
+            nc.sync.dma_start(w3_raw[b][:], w3[512 * b : 512 * b + 512].rearrange("(p j) n -> p j n", j=4))
+        w4_codes = tile([P, 2, N], U32, "w4_codes", "window2")
+        nc.sync.dma_start(w4_codes[:].bitcast(I32), w4_words.rearrange("b p c i -> p b (c i)").bitcast(I32))
+        w4_scale = planes[1][:, S : S + 2 * N].rearrange("p (b c) -> p b c", b=2)
         for q in range(4):
             nc.sync.dma_start(
                 w4_scale[32 * q : 32 * q + 4].bitcast(I32),
                 w4_scales[:, 4 * q : 4 * q + 4, :].rearrange("b r c -> r b c").bitcast(I32),
             )
 
-        for t in range(4):
-            link_slice(0, t)
-            minus_z(0, t, 0, R, zneg0[:, t, :])
-            if t in (1, 2):
-                round_w2(1, t - 1, False)
-            buy_slice(4 + t, buyer2_1[:, t, :])
-        w4_codes = tile([P, 2, N], U32, "w4_codes", "window5")
-        nc.sync.dma_start(w4_codes[:].bitcast(I32), w4_words.rearrange("b p c i -> p b (c i)").bitcast(I32))
+        def link_pair(b, t0):
+            link[b, t0], link[b, t0 + 1] = first_stage(link_job(b, t0), link_job(b, t0 + 1))
+            pick_device(b, t0)
+            pick_device(b, t0 + 1)
+
+        for t0 in (0, 2):
+            link_pair(0, t0)
+            for t in (t0, t0 + 1):
+                minus_z(0, t, 0, R, zneg0[:, t, :])
+            if t0 == 0:
+                round_w2(1)
         for t in range(4):
             link_slice(1, t)
 
-        w3_round = tile([P, 2, 2048], BF16, "w3_round", "stage_b")
-        w3q = []
-        for b in range(2):
-            dst, src = weave_views(w3_round[:, b, :], w3_raw[:, b])
-            nc.scalar.activation(dst, src, ACT.Copy)
-            w3q.append(quantise(w3_round[:, b, :], N, "w3q%d" % b))
-
-        z0_round = tile([P, 4 * R], BF16, "z0_round", "stage_c")
+        z0_round = tile([P, 4 * R], BF16, "z0_round")
         dst, src = weave_views(z0_round[:], zneg0[:])
         nc.scalar.activation(dst, src, ACT.Copy, scale=-0.5)
         zq0 = quantise(z0_round[:], R, "zq0")
+
+        w3q = []
+        for b in range(2):
+            w3_round = tile([P, 2048], BF16, "w3_round%d" % b)
+            dst, src = weave_views(w3_round[:], w3_raw[b][:])
+            nc.scalar.activation(dst, src, ACT.Copy)
+            w3q.append(quantise(w3_round[:], N, "w3q%d" % b))
 
         def regions(first_bank, width):
             per_bank = BANK // width
@@ -251,17 +271,14 @@ def tile_list_refund_ring_links_kernel(
             second_stage(0, zq0, m0, width, gate_at, y_at)
 
         out_view = out.rearrange("(n p) m -> p n m", p=P)
-        zneg_tags = ("stage_b", "stage_c", "z1_round0")
+        zneg_tags = ("table0", "w1_raw", "table0")
         for i, ((m0, width), (first, count, gate_at, y_at)) in enumerate(zip(CHUNKS, places)):
             zneg = tile([P, 4, width], F32, "zneg1%d" % i, zneg_tags[i])
             for t in range(4):
                 minus_z(1, t, m0, width, zneg[:, t, :])
             rounded = tile([P, 4 * width], BF16, "z1_round%d" % i)
             dst, src = weave_views(rounded[:], zneg[:])
-            if i < len(CHUNKS) - 1:
-                nc.scalar.activation(dst, src, ACT.Copy, scale=-0.5)
-            else:
-                nc.vector.tensor_scalar_mul(dst, src, -0.5)
+            nc.scalar.activation(dst, src, ACT.Copy, scale=-0.5)
             zq = quantise(rounded[:], width, "zq1%d" % i)
             second_stage(1, zq, 0, width, gate_at, y_at)
             for j in range(2):

@@ -51,6 +51,15 @@ def tile_list_refund_ring_links_kernel(
             rows = w2[512 * a : 512 * a + 512, 512 * b : 512 * b + 512]
             nc.sync.dma_start(dst, rows.rearrange("(p j) c -> p j c", j=4))
 
+        w1_raw = {}
+
+        def load_w1(b, tag):
+            w1_raw[b] = tile([P, 2, 256], U32, "w1_raw%d" % b, tag)
+            nc.sync.dma_start(
+                w1_raw[b][:].bitcast(I32),
+                w1_words[:, :, 1024 * b : 1024 * b + 1024].rearrange("a p c -> p a c").bitcast(I32),
+            )
+
         idx = load_list("idx", offs, S)
         ts_rows = tile([P, T], U8, "ts_rows")
         nc.sync.dma_start(
@@ -61,8 +70,7 @@ def tile_list_refund_ring_links_kernel(
             w1s_rows[0:32, :].bitcast(I32), w1_scales.rearrange("a q c -> (a q) c").bitcast(I32)
         )
         table = [load_table(0)]
-        w1_raw = tile([P, 2, 512], U32, "w1_raw")
-        nc.sync.dma_start(w1_raw[:].bitcast(I32), w1_words.rearrange("a p c -> p a c").bitcast(I32))
+        load_w1(0, "w1_raw0")
         p1 = load_list("p1", pos1, R)
         p2 = load_list("p2", pos2, R)
         p3 = load_list("p3", pos3, R)
@@ -82,30 +90,35 @@ def tile_list_refund_ring_links_kernel(
         ts_picked = tile([P, S], U8, "ts_picked")
         nc.vector.tensor_copy(ts_picked[:], ts_rows[:].indirect(idx[:]))
         nc.vector.tensor_copy(scale_rows[:, 0:S].bitcast(I32), ts_picked[:].bitcast(I32))
-        for a, q, queue in (
-            (0, 1, nc.gpsimd), (0, 2, nc.scalar), (0, 3, nc.scalar),
-            (1, 0, nc.sync), (1, 1, nc.sync), (1, 2, nc.sync), (1, 3, nc.sync),
-        ):
-            queue.dma_start(
-                planes[a][32 * q : 32 * q + 4, :].bitcast(I32),
-                scale_rows[16 * a + 4 * q : 16 * a + 4 * q + 4, :].bitcast(I32),
-            )
+        for a in (1, 0):
+            for q in range(1 - a, 4):
+                nc.sync.dma_start(
+                    planes[a][32 * q : 32 * q + 4, :].bitcast(I32),
+                    scale_rows[16 * a + 4 * q : 16 * a + 4 * q + 4, :].bitcast(I32),
+                )
 
+        load_w1(1, "ts_picked")
         v_words = [[tile([P, BANK], U32, "v_words%d%d" % (a, h)) for h in range(2)] for a in range(2)]
 
         def pick_words(a):
             for h in range(2):
                 nc.vector.tensor_copy(v_words[a][h][:], table[a][:].indirect(idx[:, 32 * h : 32 * h + 32]))
 
-        pick_words(0)
-        w1_codes = tile([P, 4 * H], U8, "w1_codes")
-        nc.vector.tensor_copy(
-            w1_codes[:].bitcast(U16).rearrange("p (g t m) -> p g t m", t=4, m=P),
-            w1_raw[:].rearrange("p a c -> p (a c)").bitcast(U16).rearrange("p (g m t) -> p g t m", t=4, m=P),
-        )
-        pick_words(1)
+        w1_codes = {}
 
-        w2_raw = {(0, 0): tile([P, 4, 512], F32, "w2_raw00", "table0"), (0, 1): tile([P, 4, 512], F32, "w2_raw01", "w1_raw")}
+        def order_w1(b):
+            w1_codes[b] = tile([P, 2048], U8, "w1_codes%d" % b)
+            nc.vector.tensor_copy(
+                w1_codes[b][:].bitcast(U16).rearrange("p (a t m) -> p a t m", t=4, m=P),
+                w1_raw[b][:].rearrange("p a c -> p (a c)").bitcast(U16).rearrange("p (a m t) -> p a t m", t=4, m=P),
+            )
+
+        pick_words(0)
+        order_w1(0)
+        pick_words(1)
+        order_w1(1)
+
+        w2_raw = {(0, 0): tile([P, 4, 512], F32, "w2_raw00", "table0"), (0, 1): tile([P, 4, 512], F32, "w2_raw01", "w1_raw0")}
         load_w2(0, 0, w2_raw[0, 0][:])
         load_w2(0, 1, w2_raw[0, 1][:])
         w2_raw1 = tile([P, 2, 4, 512], F32, "w2_raw1", "table1")
@@ -165,8 +178,8 @@ def tile_list_refund_ring_links_kernel(
 
         def buy_job(s):
             def w1_slice(a):
-                c = H * a + P * s
-                return w1_codes[:, 2 * c : 2 * c + 2 * P].bitcast(FP4X4), planes[a][:, S + P * s : S + P * s + P]
+                c = 512 * a + P * (s % 4)
+                return w1_codes[s // 4][:, 2 * c : 2 * c + 2 * P].bitcast(FP4X4), planes[a][:, S + P * s : S + P * s + P]
 
             return w1_slice, ACT.Square
 
@@ -203,7 +216,7 @@ def tile_list_refund_ring_links_kernel(
         for s in range(8):
             buy_slice(s, buyer2_all[:, s, :])
 
-        w3_raw = [tile([P, 4, N], F32, "w3_raw%d" % b, tag) for b, tag in enumerate(("table0", "w1_raw"))]
+        w3_raw = [tile([P, 4, N], F32, "w3_raw%d" % b, tag) for b, tag in enumerate(("table0", "w1_raw0"))]
         for b in range(2):
             nc.sync.dma_start(w3_raw[b][:], w3[512 * b : 512 * b + 512].rearrange("(p j) n -> p j n", j=4))
         w4_codes = tile([P, 2, N], U32, "w4_codes", "window2")
@@ -271,7 +284,7 @@ def tile_list_refund_ring_links_kernel(
             second_stage(0, zq0, m0, width, gate_at, y_at)
 
         out_view = out.rearrange("(n p) m -> p n m", p=P)
-        zneg_tags = ("table0", "w1_raw", "table0")
+        zneg_tags = ("table0", "w1_raw0", "table0")
         for i, ((m0, width), (first, count, gate_at, y_at)) in enumerate(zip(CHUNKS, places)):
             zneg = tile([P, 4, width], F32, "zneg1%d" % i, zneg_tags[i])
             for t in range(4):

@@ -118,8 +118,12 @@ def tile_list_refund_ring_links_kernel(
         pick_words(1)
         order_w1(1)
 
-        w2_raw = {(0, 0): tile([P, 4, 512], F32, "w2_raw00", "table0"), (0, 1): tile([P, 4, 512], F32, "w2_raw01", "w1_raw0")}
-        load_w2(0, 0, w2_raw[0, 0][:])
+        w2_raw00 = tile([P, 2, 4, 256], F32, "w2_raw00", "table0")
+        w2_first = [w2_raw00[:, half] for half in range(2)]
+        for half in range(2):
+            rows = w2[0:512, 256 * half : 256 * half + 256]
+            nc.sync.dma_start(w2_first[half], rows.rearrange("(p j) c -> p j c", j=4))
+        w2_raw = {(0, 1): tile([P, 4, 512], F32, "w2_raw01", "w1_raw0")}
         load_w2(0, 1, w2_raw[0, 1][:])
         w2_raw1 = tile([P, 2, 4, 512], F32, "w2_raw1", "table1")
         for a in range(2):
@@ -157,19 +161,24 @@ def tile_list_refund_ring_links_kernel(
 
         w2q = {}
 
-        def round_w2(b):
-            rounded = tile([P, 2, 2048], BF16, "w2_round%d" % b, "w2_round")
-            for a in range(2):
-                dst = rounded[:, a].rearrange("p (t m j) -> p m j t", t=4, j=4)
-                src = w2_raw[b, a][:].rearrange("p j (m t) -> p m j t", t=4)
-                if b == 0:
-                    nc.gpsimd.tensor_scalar(
-                        dst.rearrange("p m j t -> p m t j"), src.rearrange("p m j t -> p m t j"),
-                        1.0, 0.0, ALU.mult, ALU.add,
-                    )
-                else:
-                    nc.scalar.activation(dst, src, ACT.Copy)
-            w2q[b] = quantise(rounded[:].rearrange("p a c -> p (a c)"), 1024, "w2q%d" % b)
+        w2_round = {}
+
+        def round_w2(b, a):
+            if a == 0:
+                w2_round[b] = tile([P, 2, 2048], BF16, "w2_round%d" % b, "w2_round")
+            dst = w2_round[b][:, a].rearrange("p (t m j) -> p m t j", t=4, j=4)
+            if (b, a) == (0, 0):
+                for half in range(2):
+                    src = w2_first[half][:].rearrange("p j (m t) -> p m t j", t=4)
+                    nc.gpsimd.tensor_scalar(dst[:, 64 * half : 64 * half + 64], src, 1.0, 0.0, ALU.mult, ALU.add)
+                return
+            src = w2_raw[b, a][:].rearrange("p j (m t) -> p m t j", t=4)
+            if (b, a) != (1, 1):
+                nc.gpsimd.tensor_scalar(dst, src, 1.0, 0.0, ALU.mult, ALU.add)
+            else:
+                nc.scalar.activation(dst.rearrange("p m t j -> p m j t"), src.rearrange("p m t j -> p m j t"), ACT.Copy)
+            if a == 1:
+                w2q[b] = quantise(w2_round[b][:].rearrange("p a c -> p (a c)"), 1024, "w2q%d" % b)
 
         buyer2 = {}
         link = {}
@@ -212,7 +221,9 @@ def tile_list_refund_ring_links_kernel(
             )
 
         buyer2_all = tile([P, 8, R], F32, "buyer2_all")
-        round_w2(0)
+        round_w2(0, 0)
+        round_w2(0, 1)
+        round_w2(1, 0)
         for s in range(8):
             buy_slice(s, buyer2_all[:, s, :])
 
@@ -238,7 +249,7 @@ def tile_list_refund_ring_links_kernel(
             for t in (t0, t0 + 1):
                 minus_z(0, t, 0, R, zneg0[:, t, :])
             if t0 == 0:
-                round_w2(1)
+                round_w2(1, 1)
         for t in range(4):
             link_slice(1, t)
 
@@ -291,7 +302,10 @@ def tile_list_refund_ring_links_kernel(
                 minus_z(1, t, m0, width, zneg[:, t, :])
             rounded = tile([P, 4 * width], BF16, "z1_round%d" % i)
             dst, src = weave_views(rounded[:], zneg[:])
-            nc.scalar.activation(dst, src, ACT.Copy, scale=-0.5)
+            if i == 2:
+                nc.vector.tensor_scalar_mul(dst, src, -0.5)
+            else:
+                nc.scalar.activation(dst, src, ACT.Copy, scale=-0.5)
             zq = quantise(rounded[:], width, "zq1%d" % i)
             second_stage(1, zq, 0, width, gate_at, y_at)
             for j in range(2):
@@ -304,7 +318,7 @@ def tile_list_refund_ring_links_kernel(
                 nc.vector.scalar_tensor_tensor(
                     res[:], gate[:], 1.0, banks[first + count + k][:, cols], ALU.add, ALU.mult
                 )
-                nc.sync.dma_start(
+                (nc.scalar if (i, j) == (2, 0) else nc.sync).dma_start(
                     out_view[:, 2 * j : 2 * j + 2, m0 : m0 + width],
                     res[:].rearrange("p (n m) -> p n m", m=width),
                 )

@@ -115,6 +115,11 @@ def tile_list_refund_ring_links_kernel(
 
         pick_words(0)
         order_w1(0)
+        for i in range(8):
+            nc.tensor.matmul_mx(
+                banks[7][:], lhsT=w1_codes[0][:, 0 : 2 * P].bitcast(FP4X4), lhsT_scale=w1s_rows[:, 0:P],
+                rhs=v_words[0][0][:].bitcast(FP8X4), rhs_scale=w1s_rows[:, 0:BANK], start=True, stop=True,
+            )
         pick_words(1)
         order_w1(1)
 

@@ -140,7 +140,7 @@ def tile_list_refund_ring_links_kernel(
         def first_stage(*jobs):
             windows = []
             for job in jobs:
-                windows.append(tile([P, S], F32, "window%d" % len(made)))
+                windows.append(tile([P, S], F32, "window%d" % len(made), "table0" if len(made) == 12 else None))
                 made.append(windows[-1])
             for h in range(2):
                 for i, (lhs, func) in enumerate(jobs):
@@ -255,20 +255,24 @@ def tile_list_refund_ring_links_kernel(
                 minus_z(0, t, 0, R, zneg0[:, t, :])
             if t0 == 0:
                 round_w2(1, 1)
-        for t in range(4):
-            link_slice(1, t)
-
-        z0_round = tile([P, 4 * R], BF16, "z0_round")
-        dst, src = weave_views(z0_round[:], zneg0[:])
-        nc.scalar.activation(dst, src, ACT.Copy, scale=-0.5)
-        zq0 = quantise(z0_round[:], R, "zq0")
-
         w3q = []
-        for b in range(2):
+
+        def quantise_w3(b):
             w3_round = tile([P, 2048], BF16, "w3_round%d" % b)
             dst, src = weave_views(w3_round[:], w3_raw[b][:])
             nc.scalar.activation(dst, src, ACT.Copy)
             w3q.append(quantise(w3_round[:], N, "w3q%d" % b))
+
+        quantise_w3(0)
+        for t in range(4):
+            link_slice(1, t)
+
+        z0_round = tile([P, 4 * R], BF16, "z0_round", "w2q1_codes")
+        dst, src = weave_views(z0_round[:], zneg0[:])
+        nc.scalar.activation(dst, src, ACT.Copy, scale=-0.5)
+        zq0 = quantise(z0_round[:], R, "zq0")
+
+        quantise_w3(1)
 
         def regions(first_bank, width):
             per_bank = BANK // width
@@ -300,7 +304,7 @@ def tile_list_refund_ring_links_kernel(
             second_stage(0, zq0, m0, width, gate_at, y_at)
 
         out_view = out.rearrange("(n p) m -> p n m", p=P)
-        zneg_tags = ("table0", "w1_raw0", "table0")
+        zneg_tags = ("zneg0", "w1_raw0", "zneg0")
         for i, ((m0, width), (first, count, gate_at, y_at)) in enumerate(zip(CHUNKS, places)):
             zneg = tile([P, 4, width], F32, "zneg1%d" % i, zneg_tags[i])
             for t in range(4):

@@ -115,7 +115,7 @@ def tile_list_refund_ring_links_kernel(
 
         pick_words(0)
         order_w1(0)
-        for i in range(8):
+        for i in range(6):
             nc.tensor.matmul_mx(
                 banks[7][:], lhsT=w1_codes[0][:, 0 : 2 * P].bitcast(FP4X4), lhsT_scale=w1s_rows[:, 0:P],
                 rhs=v_words[0][0][:].bitcast(FP8X4), rhs_scale=w1s_rows[:, 0:BANK], start=True, stop=True,
@@ -152,7 +152,10 @@ def tile_list_refund_ring_links_kernel(
                             rhs=v_words[a][h][:].bitcast(FP8X4), rhs_scale=planes[a][:, BANK * h : BANK * h + BANK],
                             start=(a == 0), stop=(a == 1),
                         )
-                    nc.scalar.activation(windows[i][:, BANK * h : BANK * h + BANK], bank[:], func)
+                    if func == ACT.Copy:
+                        nc.scalar.copy(windows[i][:, BANK * h : BANK * h + BANK], bank[:])
+                    else:
+                        nc.scalar.activation(windows[i][:, BANK * h : BANK * h + BANK], bank[:], func)
             return windows
 
         def quantise(rounded, width, name):
@@ -166,24 +169,32 @@ def tile_list_refund_ring_links_kernel(
 
         w2q = {}
 
-        w2_round = {}
+        def round_first_block():
+            rounded = tile([P, 4096], BF16, "w2_round0", "w2_round")
+            dst = rounded[:].rearrange("p (t a m j) -> p a m t j", t=4, a=2, j=4)
+            for half in range(2):
+                src = w2_first[half][:].rearrange("p j (m t) -> p m t j", t=4)
+                nc.gpsimd.tensor_scalar(dst[:, 0, 64 * half : 64 * half + 64], src, 1.0, 0.0, ALU.mult, ALU.add)
+            src = w2_raw[0, 1][:].rearrange("p j (m t) -> p m t j", t=4)
+            nc.gpsimd.tensor_scalar(dst[:, 1], src, 1.0, 0.0, ALU.mult, ALU.add)
+            for pair in range(2):
+                codes, scale = quantise(rounded[:, 2048 * pair : 2048 * pair + 2048], BANK, "w2q0%d" % pair)
+                for t in range(2):
+                    for a in range(2):
+                        cols = slice(P * (2 * t + a), P * (2 * t + a) + P)
+                        w2q[0, 2 * pair + t, a] = codes[:, cols], scale[:, cols]
 
-        def round_w2(b, a):
+        def round_second_block(a):
+            rounded = tile([P, 2048], BF16, "w2_round1%d" % a, ("w2_round", "w2q00_codes")[a])
+            dst = rounded[:].rearrange("p (t m j) -> p m t j", t=4, j=4)
+            src = w2_raw[1, a][:].rearrange("p j (m t) -> p m t j", t=4)
             if a == 0:
-                w2_round[b] = tile([P, 2, 2048], BF16, "w2_round%d" % b, "w2_round")
-            dst = w2_round[b][:, a].rearrange("p (t m j) -> p m t j", t=4, j=4)
-            if (b, a) == (0, 0):
-                for half in range(2):
-                    src = w2_first[half][:].rearrange("p j (m t) -> p m t j", t=4)
-                    nc.gpsimd.tensor_scalar(dst[:, 64 * half : 64 * half + 64], src, 1.0, 0.0, ALU.mult, ALU.add)
-                return
-            src = w2_raw[b, a][:].rearrange("p j (m t) -> p m t j", t=4)
-            if (b, a) != (1, 1):
                 nc.gpsimd.tensor_scalar(dst, src, 1.0, 0.0, ALU.mult, ALU.add)
             else:
                 nc.scalar.activation(dst.rearrange("p m t j -> p m j t"), src.rearrange("p m t j -> p m j t"), ACT.Copy)
-            if a == 1:
-                w2q[b] = quantise(w2_round[b][:].rearrange("p a c -> p (a c)"), 1024, "w2q%d" % b)
+            codes, scale = quantise(rounded[:], BANK, "w2q1%d" % a)
+            for t in range(4):
+                w2q[1, t, a] = codes[:, P * t : P * t + P], scale[:, P * t : P * t + P]
 
         buyer2 = {}
         link = {}
@@ -199,9 +210,8 @@ def tile_list_refund_ring_links_kernel(
 
         def link_job(b, t):
             def w2_slice(a):
-                codes, scale = w2q[b]
-                cols = slice(512 * a + P * t, 512 * a + P * t + P)
-                return codes[:, cols].bitcast(FP8X4), scale[:, cols]
+                codes, scale = w2q[b, t, a]
+                return codes.bitcast(FP8X4), scale
 
             return w2_slice, ACT.Copy
 
@@ -226,9 +236,8 @@ def tile_list_refund_ring_links_kernel(
             )
 
         buyer2_all = tile([P, 8, R], F32, "buyer2_all")
-        round_w2(0, 0)
-        round_w2(0, 1)
-        round_w2(1, 0)
+        round_first_block()
+        round_second_block(0)
         for s in range(8):
             buy_slice(s, buyer2_all[:, s, :])
 
@@ -254,7 +263,7 @@ def tile_list_refund_ring_links_kernel(
             for t in (t0, t0 + 1):
                 minus_z(0, t, 0, R, zneg0[:, t, :])
             if t0 == 0:
-                round_w2(1, 1)
+                round_second_block(1)
         w3q = []
 
         def quantise_w3(b):
@@ -267,7 +276,7 @@ def tile_list_refund_ring_links_kernel(
         for t in range(4):
             link_slice(1, t)
 
-        z0_round = tile([P, 4 * R], BF16, "z0_round", "w2q1_codes")
+        z0_round = tile([P, 4 * R], BF16, "z0_round", "w2q11_codes")
         dst, src = weave_views(z0_round[:], zneg0[:])
         nc.scalar.activation(dst, src, ACT.Copy, scale=-0.5)
         zq0 = quantise(z0_round[:], R, "zq0")

@@ -124,39 +124,34 @@ def tile_list_refund_ring_links_kernel(
         order_w1(1)
 
         w2_raw00 = tile([P, 2, 4, 256], F32, "w2_raw00", "table0")
-        w2_first = [w2_raw00[:, half] for half in range(2)]
         for half in range(2):
             rows = w2[0:512, 256 * half : 256 * half + 256]
-            nc.sync.dma_start(w2_first[half], rows.rearrange("(p j) c -> p j c", j=4))
-        w2_raw = {(0, 1): tile([P, 4, 512], F32, "w2_raw01", "w1_raw0")}
-        load_w2(0, 1, w2_raw[0, 1][:])
+            nc.sync.dma_start(w2_raw00[:, half], rows.rearrange("(p j) c -> p j c", j=4))
+        w2_raw01 = tile([P, 4, 512], F32, "w2_raw01", "w1_raw0")
+        load_w2(0, 1, w2_raw01[:])
         w2_raw1 = tile([P, 2, 4, 512], F32, "w2_raw1", "table1")
         for a in range(2):
-            w2_raw[1, a] = w2_raw1[:, a]
             load_w2(1, a, w2_raw1[:, a])
 
-        made = []
+        filled = []
 
-        def first_stage(*jobs):
-            windows = []
-            for job in jobs:
-                windows.append(tile([P, S], F32, "window%d" % len(made), "table0" if len(made) == 12 else None))
-                made.append(windows[-1])
+        def first_stage(lhs, func, tag):
+            window = tile([P, S], F32, "window%d" % len(filled), tag)
             for h in range(2):
-                for i, (lhs, func) in enumerate(jobs):
-                    bank = banks[(2 * (len(made) - len(jobs)) + len(jobs) * h + i) % 8]
-                    for a in range(2):
-                        codes, scale = lhs(a)
-                        nc.tensor.matmul_mx(
-                            bank[:], lhsT=codes, lhsT_scale=scale,
-                            rhs=v_words[a][h][:].bitcast(FP8X4), rhs_scale=planes[a][:, BANK * h : BANK * h + BANK],
-                            start=(a == 0), stop=(a == 1),
-                        )
-                    if func == ACT.Copy:
-                        nc.scalar.copy(windows[i][:, BANK * h : BANK * h + BANK], bank[:])
-                    else:
-                        nc.scalar.activation(windows[i][:, BANK * h : BANK * h + BANK], bank[:], func)
-            return windows
+                bank = banks[(2 * len(filled) + h) % 8]
+                for a in range(2):
+                    codes, scale = lhs(a)
+                    nc.tensor.matmul_mx(
+                        bank[:], lhsT=codes, lhsT_scale=scale,
+                        rhs=v_words[a][h][:].bitcast(FP8X4), rhs_scale=planes[a][:, BANK * h : BANK * h + BANK],
+                        start=(a == 0), stop=(a == 1),
+                    )
+                if func == ACT.Copy:
+                    nc.scalar.copy(window[:, BANK * h : BANK * h + BANK], bank[:])
+                else:
+                    nc.scalar.activation(window[:, BANK * h : BANK * h + BANK], bank[:], func)
+            filled.append(window)
+            return window
 
         def quantise(rounded, width, name):
             codes = tile([P, width], U32, name + "_codes")
@@ -164,87 +159,44 @@ def tile_list_refund_ring_links_kernel(
             nc.vector.quantize_mx(out=codes[:].bitcast(FP8X4), scales=scale[:], in_=rounded)
             return codes, scale
 
-        def weave_views(dst, raw):
-            return dst.rearrange("p (c i j) -> p c j i", i=4, j=4), raw.rearrange("p j (c i) -> p c j i", i=4)
+        def woven(dst, run):
+            return dst.rearrange("p (c i j) -> p c j i", i=run, j=4)
+
+        def by_rows(src, run):
+            return src.rearrange("p j (c i) -> p c j i", i=run)
 
         w2q = {}
 
-        def round_first_block():
-            rounded = tile([P, 4096], BF16, "w2_round0", "w2_round")
+        def round_w2(b, pieces):
+            rounded = tile([P, 4096], BF16, "w2_round%d" % b, "w2_round")
             dst = rounded[:].rearrange("p (t a m j) -> p a m t j", t=4, a=2, j=4)
-            for half in range(2):
-                src = w2_first[half][:].rearrange("p j (m t) -> p m t j", t=4)
-                nc.gpsimd.tensor_scalar(dst[:, 0, 64 * half : 64 * half + 64], src, 1.0, 0.0, ALU.mult, ALU.add)
-            src = w2_raw[0, 1][:].rearrange("p j (m t) -> p m t j", t=4)
-            nc.gpsimd.tensor_scalar(dst[:, 1], src, 1.0, 0.0, ALU.mult, ALU.add)
+            for a, m0, raw in pieces:
+                src = raw.rearrange("p j (m t) -> p m t j", t=4)
+                nc.gpsimd.tensor_scalar(dst[:, a, m0 : m0 + src.shape[1]], src, 1.0, 0.0, ALU.mult, ALU.add)
             for pair in range(2):
-                codes, scale = quantise(rounded[:, 2048 * pair : 2048 * pair + 2048], BANK, "w2q0%d" % pair)
+                codes, scale = quantise(rounded[:, 2048 * pair : 2048 * pair + 2048], BANK, "w2q%d%d" % (b, pair))
                 for t in range(2):
                     for a in range(2):
                         cols = slice(P * (2 * t + a), P * (2 * t + a) + P)
-                        w2q[0, 2 * pair + t, a] = codes[:, cols], scale[:, cols]
+                        w2q[b, 2 * pair + t, a] = codes[:, cols].bitcast(FP8X4), scale[:, cols]
 
-        def round_second_block(a):
-            rounded = tile([P, 2048], BF16, "w2_round1%d" % a, ("w2_round", "w2q00_codes")[a])
-            dst = rounded[:].rearrange("p (t m j) -> p m t j", t=4, j=4)
-            src = w2_raw[1, a][:].rearrange("p j (m t) -> p m t j", t=4)
-            if a == 0:
-                nc.gpsimd.tensor_scalar(dst, src, 1.0, 0.0, ALU.mult, ALU.add)
-            else:
-                nc.scalar.activation(dst.rearrange("p m t j -> p m j t"), src.rearrange("p m t j -> p m j t"), ACT.Copy)
-            codes, scale = quantise(rounded[:], BANK, "w2q1%d" % a)
-            for t in range(4):
-                w2q[1, t, a] = codes[:, P * t : P * t + P], scale[:, P * t : P * t + P]
+        round_w2(0, [(0, 0, w2_raw00[:, 0]), (0, 64, w2_raw00[:, 1]), (1, 0, w2_raw01[:])])
 
-        buyer2 = {}
-        link = {}
-        zneg0 = tile([P, 4, R], F32, "zneg0")
-        prod = [tile([P, 4, R], F32, "prod%d" % b) for b in range(2)]
-
-        def buy_job(s):
+        buyer2 = tile([P, 8, R], F32, "buyer2")
+        for s in range(8):
             def w1_slice(a):
                 c = 512 * a + P * (s % 4)
                 return w1_codes[s // 4][:, 2 * c : 2 * c + 2 * P].bitcast(FP4X4), planes[a][:, S + P * s : S + P * s + P]
 
-            return w1_slice, ACT.Square
+            window = first_stage(w1_slice, ACT.Square, None)
+            nc.vector.tensor_copy(buyer2[:, s, :], window[:].indirect(p1[:]))
 
-        def link_job(b, t):
-            def w2_slice(a):
-                codes, scale = w2q[b, t, a]
-                return codes.bitcast(FP8X4), scale
-
-            return w2_slice, ACT.Copy
-
-        def pick_buyer(s, window, dst):
-            nc.vector.tensor_copy(dst, window[:].indirect(p1[:]))
-            buyer2[s] = dst
-
-        def pick_device(b, t):
-            nc.vector.tensor_tensor(prod[b][:, t, :], link[b, t][:].indirect(p2[:]), buyer2[4 * b + t], ALU.mult)
-
-        def buy_slice(s, dst):
-            pick_buyer(s, first_stage(buy_job(s))[0], dst)
-
-        def link_slice(b, t):
-            link[b, t] = first_stage(link_job(b, t))[0]
-            pick_device(b, t)
-
-        def minus_z(b, t, m0, width, dst):
-            nc.vector.tensor_tensor(
-                dst, link[b, t][:].indirect(p3[:, m0 // 16 : (m0 + width) // 16]),
-                prod[b][:, t, m0 : m0 + width], ALU.subtract,
-            )
-
-        buyer2_all = tile([P, 8, R], F32, "buyer2_all")
-        round_first_block()
-        round_second_block(0)
-        for s in range(8):
-            buy_slice(s, buyer2_all[:, s, :])
+        round_w2(1, [(a, 0, w2_raw1[:, a]) for a in range(2)])
 
         w3_raw = [tile([P, 4, N], F32, "w3_raw%d" % b, tag) for b, tag in enumerate(("table0", "w1_raw0"))]
         for b in range(2):
             nc.sync.dma_start(w3_raw[b][:], w3[512 * b : 512 * b + 512].rearrange("(p j) n -> p j n", j=4))
-        w4_codes = tile([P, 2, N], U32, "w4_codes", "window2")
+        w4_codes = tile([P, 2, N], U32, "w4_codes", "window4")
         nc.sync.dma_start(w4_codes[:].bitcast(I32), w4_words.rearrange("b p c i -> p b (c i)").bitcast(I32))
         w4_scale = planes[1][:, S : S + 2 * N].rearrange("p (b c) -> p b c", b=2)
         for q in range(4):
@@ -253,35 +205,42 @@ def tile_list_refund_ring_links_kernel(
                 w4_scales[:, 4 * q : 4 * q + 4, :].rearrange("b r c -> r b c").bitcast(I32),
             )
 
-        def link_pair(b, t0):
-            link[b, t0], link[b, t0 + 1] = first_stage(link_job(b, t0), link_job(b, t0 + 1))
-            pick_device(b, t0)
-            pick_device(b, t0 + 1)
+        link = {}
+        prod = [tile([P, 4, R], F32, "prod%d" % b) for b in range(2)]
 
-        for t0 in (0, 2):
-            link_pair(0, t0)
-            for t in (t0, t0 + 1):
-                minus_z(0, t, 0, R, zneg0[:, t, :])
-            if t0 == 0:
-                round_second_block(1)
-        w3q = []
+        def link_block(b):
+            for t in range(4):
+                link[b, t] = first_stage(lambda a: w2q[b, t, a], ACT.Copy, ("window%d" % t) if b else None)
+                nc.vector.tensor_tensor(
+                    prod[b][:, t, :], link[b, t][:].indirect(p2[:]), buyer2[:, 4 * b + t, :], ALU.mult
+                )
 
-        def quantise_w3(b):
-            w3_round = tile([P, 2048], BF16, "w3_round%d" % b)
-            dst, src = weave_views(w3_round[:], w3_raw[b][:])
-            nc.scalar.activation(dst, src, ACT.Copy)
-            w3q.append(quantise(w3_round[:], N, "w3q%d" % b))
+        def pick_address(b, m0, width):
+            address = tile([P, 4, width], F32, "address%d_%d" % (b, m0))
+            for t in range(4):
+                nc.scalar.activation(
+                    address[:, t, :], link[b, t][:].indirect(p3[:, m0 // 16 : (m0 + width) // 16]), ACT.Copy
+                )
+            return address
 
-        quantise_w3(0)
-        for t in range(4):
-            link_slice(1, t)
+        def round_z(b, m0, width, address):
+            rounded = tile([P, 4 * width], BF16, "z_round%d_%d" % (b, m0))
+            nc.vector.tensor_tensor(
+                woven(rounded[:], 2), by_rows(prod[b][:, :, m0 : m0 + width], 2), by_rows(address[:], 2), ALU.subtract
+            )
+            return rounded
 
-        z0_round = tile([P, 4 * R], BF16, "z0_round", "w2q11_codes")
-        dst, src = weave_views(z0_round[:], zneg0[:])
-        nc.scalar.activation(dst, src, ACT.Copy, scale=-0.5)
+        link_block(0)
+        address0 = pick_address(0, 0, R)
+        w3_round = [tile([P, 2048], BF16, "w3_round%d" % b, tag) for b, tag in enumerate(("w2_round", None))]
+        nc.vector.tensor_scalar_mul(woven(w3_round[0][:], 4), by_rows(w3_raw[0][:], 4), 0.5)
+        z0_round = round_z(0, 0, R, address0)
+        w3q = [quantise(w3_round[0][:], N, "w3q0")]
         zq0 = quantise(z0_round[:], R, "zq0")
-
-        quantise_w3(1)
+        nc.scalar.activation(woven(w3_round[1][:], 4), by_rows(w3_raw[1][:], 4), ACT.Copy, scale=0.5)
+        link_block(1)
+        w3q.append(quantise(w3_round[1][:], N, "w3q1"))
+        address1 = [pick_address(1, m0, width) for m0, width in CHUNKS]
 
         def regions(first_bank, width):
             per_bank = BANK // width
@@ -312,26 +271,19 @@ def tile_list_refund_ring_links_kernel(
         for (m0, width), (first, count, gate_at, y_at) in zip(CHUNKS, places):
             second_stage(0, zq0, m0, width, gate_at, y_at)
 
-        out_view = out.rearrange("(n p) m -> p n m", p=P)
-        zneg_tags = ("zneg0", "w1_raw0", "zneg0")
         for i, ((m0, width), (first, count, gate_at, y_at)) in enumerate(zip(CHUNKS, places)):
-            zneg = tile([P, 4, width], F32, "zneg1%d" % i, zneg_tags[i])
-            for t in range(4):
-                minus_z(1, t, m0, width, zneg[:, t, :])
-            rounded = tile([P, 4 * width], BF16, "z1_round%d" % i)
-            dst, src = weave_views(rounded[:], zneg[:])
-            if i == 2:
-                nc.vector.tensor_scalar_mul(dst, src, -0.5)
-            else:
-                nc.scalar.activation(dst, src, ACT.Copy, scale=-0.5)
+            rounded = round_z(1, m0, width, address1[i])
             zq = quantise(rounded[:], width, "zq1%d" % i)
             second_stage(1, zq, 0, width, gate_at, y_at)
+
+        out_view = out.rearrange("(n p) m -> p n m", p=P)
+        for i, ((m0, width), (first, count, gate_at, y_at)) in enumerate(zip(CHUNKS, places)):
             for j in range(2):
                 c0 = (2 * j * width) % BANK
                 cols = slice(c0, c0 + 2 * width)
                 k = 2 * j * width // BANK
                 gate = tile([P, 2 * width], F32, "gate%d%d" % (i, j))
-                nc.scalar.activation(gate[:], banks[first + k][:, cols], ACT.Tanh)
+                nc.scalar.activation(gate[:], banks[first + k][:, cols], ACT.Tanh, scale=0.5)
                 res = tile([P, 2 * width], F32, "res%d%d" % (i, j))
                 nc.vector.scalar_tensor_tensor(
                     res[:], gate[:], 1.0, banks[first + count + k][:, cols], ALU.add, ALU.mult

@@ -191,7 +191,19 @@ def tile_list_refund_ring_links_kernel(
             window = first_stage(w1_slice, ACT.Square, None)
             nc.vector.tensor_copy(buyer2[:, s, :], window[:].indirect(p1[:]))
 
-        round_w2(1, [(a, 0, w2_raw1[:, a]) for a in range(2)])
+        def round_second_block(a):
+            rounded = tile([P, 2048], BF16, "w2_round1%d" % a, ("w2_round", "w2q00_codes")[a])
+            dst = rounded[:].rearrange("p (t m j) -> p m t j", t=4, j=4)
+            src = w2_raw1[:, a].rearrange("p j (m t) -> p m t j", t=4)
+            if a == 0:
+                nc.gpsimd.tensor_scalar(dst, src, 1.0, 0.0, ALU.mult, ALU.add)
+            else:
+                nc.scalar.activation(dst.rearrange("p m t j -> p m j t"), src.rearrange("p m t j -> p m j t"), ACT.Copy)
+            codes, scale = quantise(rounded[:], BANK, "w2q1%d" % a)
+            for t in range(4):
+                w2q[1, t, a] = codes[:, P * t : P * t + P].bitcast(FP8X4), scale[:, P * t : P * t + P]
+
+        round_second_block(0)
 
         w3_raw = [tile([P, 4, N], F32, "w3_raw%d" % b, tag) for b, tag in enumerate(("table0", "w1_raw0"))]
         for b in range(2):
@@ -214,6 +226,8 @@ def tile_list_refund_ring_links_kernel(
                 nc.vector.tensor_tensor(
                     prod[b][:, t, :], link[b, t][:].indirect(p2[:]), buyer2[:, 4 * b + t, :], ALU.mult
                 )
+                if (b, t) == (0, 1):
+                    round_second_block(1)
 
         def pick_address(b, m0, width):
             address = tile([P, 4, width], F32, "address%d_%d" % (b, m0))
@@ -232,14 +246,13 @@ def tile_list_refund_ring_links_kernel(
 
         link_block(0)
         address0 = pick_address(0, 0, R)
-        w3_round = [tile([P, 2048], BF16, "w3_round%d" % b, tag) for b, tag in enumerate(("w2_round", None))]
+        w3_round = [tile([P, 2048], BF16, "w3_round%d" % b, tag) for b, tag in enumerate(("w2_round", "w2q00_codes"))]
         nc.vector.tensor_scalar_mul(woven(w3_round[0][:], 4), by_rows(w3_raw[0][:], 4), 0.5)
+        nc.vector.tensor_scalar_mul(woven(w3_round[1][:], 4), by_rows(w3_raw[1][:], 4), 0.5)
+        w3q = [quantise(w3_round[b][:], N, "w3q%d" % b) for b in range(2)]
         z0_round = round_z(0, 0, R, address0)
-        w3q = [quantise(w3_round[0][:], N, "w3q0")]
-        zq0 = quantise(z0_round[:], R, "zq0")
-        nc.scalar.activation(woven(w3_round[1][:], 4), by_rows(w3_raw[1][:], 4), ACT.Copy, scale=0.5)
         link_block(1)
-        w3q.append(quantise(w3_round[1][:], N, "w3q1"))
+        zq0 = quantise(z0_round[:], R, "zq0")
         address1 = [pick_address(1, m0, width) for m0, width in CHUNKS]
 
         def regions(first_bank, width):

@@ -28,10 +28,14 @@ def tile_list_refund_ring_links_kernel(
     with ExitStack() as ctx:
         lists = ctx.enter_context(tc.tile_pool(name="lists", bufs=1))
         sb = ctx.enter_context(tc.tile_pool(name="sb", bufs=1))
+        reused = ctx.enter_context(tc.tile_pool(name="reused", bufs=1))
         psum = ctx.enter_context(tc.psum_pool(name="psum", bufs=1))
 
         def tile(shape, dtype, name, tag=None):
             return sb.tile(shape, dtype, name=name, tag=tag or name, align_bytes=64)
+
+        def placed(shape, dtype, name, kib):
+            return reused.tile(shape, dtype, name=name, tag=name, offset=1024 * kib, align_bytes=64)
 
         banks = [psum.tile([P, BANK], F32, name="bank%d" % i) for i in range(8)]
 
@@ -41,7 +45,7 @@ def tile_list_refund_ring_links_kernel(
             return offsets
 
         def load_table(a):
-            words = tile([P, T], U32, "table%d" % a)
+            words = placed([P, T], U32, "table%d" % a, 16 * a)
             nc.sync.dma_start(
                 words[:].bitcast(I32), tab_words[a].rearrange("p t i -> p (t i)").bitcast(I32)
             )
@@ -123,15 +127,15 @@ def tile_list_refund_ring_links_kernel(
         pick_words(1)
         order_w1(1)
 
-        w2_raw00 = tile([P, 2, 4, 256], F32, "w2_raw00", "table0")
+        w2_raw00 = [placed([P, 4, 256], F32, "w2_raw00%d" % half, 4 * half) for half in range(2)]
         for half in range(2):
             rows = w2[0:512, 256 * half : 256 * half + 256]
-            nc.sync.dma_start(w2_raw00[:, half], rows.rearrange("(p j) c -> p j c", j=4))
+            nc.sync.dma_start(w2_raw00[half][:], rows.rearrange("(p j) c -> p j c", j=4))
         w2_raw01 = tile([P, 4, 512], F32, "w2_raw01", "w1_raw0")
         load_w2(0, 1, w2_raw01[:])
-        w2_raw1 = tile([P, 2, 4, 512], F32, "w2_raw1", "table1")
+        w2_raw1 = [placed([P, 4, 512], F32, "w2_raw1%d" % a, 16 + 8 * a) for a in range(2)]
         for a in range(2):
-            load_w2(1, a, w2_raw1[:, a])
+            load_w2(1, a, w2_raw1[a][:])
 
         filled = []
 
@@ -153,8 +157,8 @@ def tile_list_refund_ring_links_kernel(
             filled.append(window)
             return window
 
-        def quantise(rounded, width, name):
-            codes = tile([P, width], U32, name + "_codes")
+        def quantise(rounded, width, name, tag=None):
+            codes = tile([P, width], U32, name + "_codes", tag)
             scale = tile([P, width], U8, name + "_scale")
             nc.vector.quantize_mx(out=codes[:].bitcast(FP8X4), scales=scale[:], in_=rounded)
             return codes, scale
@@ -180,21 +184,21 @@ def tile_list_refund_ring_links_kernel(
                         cols = slice(P * (2 * t + a), P * (2 * t + a) + P)
                         w2q[b, 2 * pair + t, a] = codes[:, cols].bitcast(FP8X4), scale[:, cols]
 
-        round_w2(0, [(0, 0, w2_raw00[:, 0]), (0, 64, w2_raw00[:, 1]), (1, 0, w2_raw01[:])])
+        round_w2(0, [(0, 0, w2_raw00[0][:]), (0, 64, w2_raw00[1][:]), (1, 0, w2_raw01[:])])
 
-        buyer2 = tile([P, 8, R], F32, "buyer2")
+        buyer2 = [tile([P, R], F32, "buyer2_%d" % s) for s in range(8)]
         for s in range(8):
             def w1_slice(a):
                 c = 512 * a + P * (s % 4)
                 return w1_codes[s // 4][:, 2 * c : 2 * c + 2 * P].bitcast(FP4X4), planes[a][:, S + P * s : S + P * s + P]
 
             window = first_stage(w1_slice, ACT.Square, None)
-            nc.vector.tensor_copy(buyer2[:, s, :], window[:].indirect(p1[:]))
+            nc.vector.tensor_copy(buyer2[s][:], window[:].indirect(p1[:]))
 
         def round_second_block(a):
             rounded = tile([P, 2048], BF16, "w2_round1%d" % a, ("w2_round", "w2q00_codes")[a])
             dst = rounded[:].rearrange("p (t m j) -> p m t j", t=4, j=4)
-            src = w2_raw1[:, a].rearrange("p j (m t) -> p m t j", t=4)
+            src = w2_raw1[a][:].rearrange("p j (m t) -> p m t j", t=4)
             if a == 0:
                 nc.gpsimd.tensor_scalar(dst, src, 1.0, 0.0, ALU.mult, ALU.add)
             else:
@@ -205,7 +209,7 @@ def tile_list_refund_ring_links_kernel(
 
         round_second_block(0)
 
-        w3_raw = [tile([P, 4, N], F32, "w3_raw%d" % b, tag) for b, tag in enumerate(("table0", "w1_raw0"))]
+        w3_raw = [placed([P, 4, N], F32, "w3_raw0", 0), tile([P, 4, N], F32, "w3_raw1", "w1_raw0")]
         for b in range(2):
             nc.sync.dma_start(w3_raw[b][:], w3[512 * b : 512 * b + 512].rearrange("(p j) n -> p j n", j=4))
         w4_codes = tile([P, 2, N], U32, "w4_codes", "window4")
@@ -220,22 +224,20 @@ def tile_list_refund_ring_links_kernel(
         link = {}
         prod = [tile([P, 4, R], F32, "prod%d" % b) for b in range(2)]
 
-        def link_block(b):
-            for t in range(4):
-                link[b, t] = first_stage(lambda a: w2q[b, t, a], ACT.Copy, ("window%d" % t) if b else None)
-                nc.vector.tensor_tensor(
-                    prod[b][:, t, :], link[b, t][:].indirect(p2[:]), buyer2[:, 4 * b + t, :], ALU.mult
-                )
-                if (b, t) == (0, 1):
-                    round_second_block(1)
+        def link_slice(b, t):
+            link[b, t] = first_stage(lambda a: w2q[b, t, a], ACT.Copy, ("window%d" % t) if b else None)
 
-        def pick_address(b, m0, width):
-            address = tile([P, 4, width], F32, "address%d_%d" % (b, m0))
-            for t in range(4):
-                nc.scalar.activation(
-                    address[:, t, :], link[b, t][:].indirect(p3[:, m0 // 16 : (m0 + width) // 16]), ACT.Copy
-                )
-            return address
+        def pick_device(b, t):
+            nc.vector.tensor_tensor(prod[b][:, t, :], link[b, t][:].indirect(p2[:]), buyer2[4 * b + t][:], ALU.mult)
+
+        address = {}
+
+        def pick_address(b, t, m0, width):
+            if (b, m0) not in address:
+                address[b, m0] = tile([P, 4, width], F32, "address%d_%d" % (b, m0))
+            nc.scalar.activation(
+                address[b, m0][:, t, :], link[b, t][:].indirect(p3[:, m0 // 16 : (m0 + width) // 16]), ACT.Copy
+            )
 
         def round_z(b, m0, width, address):
             rounded = tile([P, 4 * width], BF16, "z_round%d_%d" % (b, m0))
@@ -244,16 +246,29 @@ def tile_list_refund_ring_links_kernel(
             )
             return rounded
 
-        link_block(0)
-        address0 = pick_address(0, 0, R)
-        w3_round = [tile([P, 2048], BF16, "w3_round%d" % b, tag) for b, tag in enumerate(("w2_round", "w2q00_codes"))]
+        for t in range(4):
+            link_slice(0, t)
+            pick_device(0, t)
+            if t == 1:
+                round_second_block(1)
+        w3_round = [placed([P, 2048], BF16, "w3_round%d" % b, 16 + 8 * b) for b in range(2)]
         nc.vector.tensor_scalar_mul(woven(w3_round[0][:], 4), by_rows(w3_raw[0][:], 4), 0.5)
-        nc.vector.tensor_scalar_mul(woven(w3_round[1][:], 4), by_rows(w3_raw[1][:], 4), 0.5)
-        w3q = [quantise(w3_round[b][:], N, "w3q%d" % b) for b in range(2)]
-        z0_round = round_z(0, 0, R, address0)
-        link_block(1)
+        nc.vector.tensor_scalar_mul(woven(w3_round[1][:, 0 : 4 * 384], 4), by_rows(w3_raw[1][:, :, 0:384], 4), 0.5)
+        for t in range(4):
+            pick_address(0, t, 0, R)
+        w3q = [quantise(w3_round[0][:], N, "w3q0", "window8")]
+        z0_round = round_z(0, 0, R, address[0, 0])
+        for t in range(4):
+            link_slice(1, t)
+            pick_device(1, t)
         zq0 = quantise(z0_round[:], R, "zq0")
-        address1 = [pick_address(1, m0, width) for m0, width in CHUNKS]
+        nc.scalar.activation(
+            woven(w3_round[1][:, 4 * 384 : 4 * N], 4), by_rows(w3_raw[1][:, :, 384:N], 4), ACT.Copy, scale=0.5
+        )
+        w3q.append(quantise(w3_round[1][:], N, "w3q1"))
+        for m0, width in CHUNKS:
+            for t in range(4):
+                pick_address(1, t, m0, width)
 
         def regions(first_bank, width):
             per_bank = BANK // width
@@ -284,9 +299,11 @@ def tile_list_refund_ring_links_kernel(
         for (m0, width), (first, count, gate_at, y_at) in zip(CHUNKS, places):
             second_stage(0, zq0, m0, width, gate_at, y_at)
 
+        z1_round = [round_z(1, m0, width, address[1, m0]) for m0, width in CHUNKS[:2]]
         for i, ((m0, width), (first, count, gate_at, y_at)) in enumerate(zip(CHUNKS, places)):
-            rounded = round_z(1, m0, width, address1[i])
-            zq = quantise(rounded[:], width, "zq1%d" % i)
+            if i == 1:
+                z1_round.append(round_z(1, *CHUNKS[2], address[1, CHUNKS[2][0]]))
+            zq = quantise(z1_round[i][:], width, "zq1%d" % i)
             second_stage(1, zq, 0, width, gate_at, y_at)
 
         out_view = out.rearrange("(n p) m -> p n m", p=P)

@@ -18,6 +18,10 @@ ALU = mybir.AluOpType
 
 P = 128
 BANK = 512
+FIRST_PASSES = (
+    (0, 0, 512, 0), (0, 512, 256, 0), (0, 768, 256, 0), (0, 0, 512, 1), (0, 512, 256, 1),
+    (1, 0, 512, 1), (0, 768, 256, 1), (1, 0, 512, 0), (1, 512, 512, 1), (1, 512, 512, 0),
+)
 CHUNKS = ((0, 256), (256, 128), (384, 128))
 
 
@@ -45,7 +49,7 @@ def tile_list_refund_ring_links_kernel(
             return offsets
 
         def load_table(a):
-            words = placed([P, T], U32, "table%d" % a, 16 * a)
+            words = placed([P, T], U32, "table%d" % a, 2 + 16 * a)
             nc.sync.dma_start(
                 words[:].bitcast(I32), tab_words[a].rearrange("p t i -> p (t i)").bitcast(I32)
             )
@@ -94,7 +98,7 @@ def tile_list_refund_ring_links_kernel(
         ts_picked = tile([P, S], U8, "ts_picked")
         nc.vector.tensor_copy(ts_picked[:], ts_rows[:].indirect(idx[:]))
         nc.vector.tensor_copy(scale_rows[:, 0:S].bitcast(I32), ts_picked[:].bitcast(I32))
-        for a in (1, 0):
+        for a in (0, 1):
             for q in range(1 - a, 4):
                 nc.sync.dma_start(
                     planes[a][32 * q : 32 * q + 4, :].bitcast(I32),
@@ -105,8 +109,11 @@ def tile_list_refund_ring_links_kernel(
         v_words = [[tile([P, BANK], U32, "v_words%d%d" % (a, h)) for h in range(2)] for a in range(2)]
 
         def pick_words(a):
-            for h in range(2):
-                nc.vector.tensor_copy(v_words[a][h][:], table[a][:].indirect(idx[:, 32 * h : 32 * h + 32]))
+            for j0, width in ((0, 512), (512, 512)) if a == 0 else ((0, 512), (512, 256), (768, 256)):
+                nc.vector.tensor_copy(
+                    v_words[a][j0 // BANK][:, j0 % BANK : j0 % BANK + width],
+                    table[a][:].indirect(idx[:, j0 // 16 : (j0 + width) // 16]),
+                )
 
         w1_codes = {}
 
@@ -119,7 +126,7 @@ def tile_list_refund_ring_links_kernel(
 
         pick_words(0)
         order_w1(0)
-        for i in range(6):
+        for i in range(5):
             nc.tensor.matmul_mx(
                 banks[7][:], lhsT=w1_codes[0][:, 0 : 2 * P].bitcast(FP4X4), lhsT_scale=w1s_rows[:, 0:P],
                 rhs=v_words[0][0][:].bitcast(FP8X4), rhs_scale=w1s_rows[:, 0:BANK], start=True, stop=True,
@@ -131,29 +138,43 @@ def tile_list_refund_ring_links_kernel(
         for half in range(2):
             rows = w2[0:512, 256 * half : 256 * half + 256]
             nc.sync.dma_start(w2_raw00[half][:], rows.rearrange("(p j) c -> p j c", j=4))
-        w2_raw01 = tile([P, 4, 512], F32, "w2_raw01", "w1_raw0")
+        w2_raw01 = placed([P, 4, 512], F32, "w2_raw01", 8)
         load_w2(0, 1, w2_raw01[:])
-        w2_raw1 = [placed([P, 4, 512], F32, "w2_raw1%d" % a, 16 + 8 * a) for a in range(2)]
+        w2_raw1 = [placed([P, 4, 512], F32, "w2_raw1%d" % a, 18 + 8 * a) for a in range(2)]
         for a in range(2):
             load_w2(1, a, w2_raw1[a][:])
 
         filled = []
 
+        used = []
+
+        def next_bank():
+            used.append(banks[len(used) % 8])
+            return used[-1]
+
+        def multiply(bank, lhs, j0, width, a, first):
+            codes, scale = lhs(a)
+            nc.tensor.matmul_mx(
+                bank[:, 0:width], lhsT=codes, lhsT_scale=scale,
+                rhs=v_words[a][j0 // BANK][:, j0 % BANK : j0 % BANK + width].bitcast(FP8X4),
+                rhs_scale=planes[a][:, j0 : j0 + width],
+                start=first, stop=not first,
+            )
+
+        def empty(window, j0, sums, func):
+            dst = window[:, j0 : j0 + sums.shape[1]]
+            if func == ACT.Copy:
+                nc.scalar.copy(dst, sums)
+            else:
+                nc.scalar.activation(dst, sums, func)
+
         def first_stage(lhs, func, tag):
             window = tile([P, S], F32, "window%d" % len(filled), tag)
-            for h in range(2):
-                bank = banks[(2 * len(filled) + h) % 8]
-                for a in range(2):
-                    codes, scale = lhs(a)
-                    nc.tensor.matmul_mx(
-                        bank[:], lhsT=codes, lhsT_scale=scale,
-                        rhs=v_words[a][h][:].bitcast(FP8X4), rhs_scale=planes[a][:, BANK * h : BANK * h + BANK],
-                        start=(a == 0), stop=(a == 1),
-                    )
-                if func == ACT.Copy:
-                    nc.scalar.copy(window[:, BANK * h : BANK * h + BANK], bank[:])
-                else:
-                    nc.scalar.activation(window[:, BANK * h : BANK * h + BANK], bank[:], func)
+            for j0 in (0, BANK):
+                bank = next_bank()
+                for a in (1, 0):
+                    multiply(bank, lhs, j0, BANK, a, a == 1)
+                empty(window, j0, bank[:], func)
             filled.append(window)
             return window
 
@@ -186,13 +207,26 @@ def tile_list_refund_ring_links_kernel(
 
         round_w2(0, [(0, 0, w2_raw00[0][:]), (0, 64, w2_raw00[1][:]), (1, 0, w2_raw01[:])])
 
-        buyer2 = [tile([P, R], F32, "buyer2_%d" % s) for s in range(8)]
-        for s in range(8):
-            def w1_slice(a):
+        buyer2 = [(placed([P, R], F32, "buyer2_5", 8) if s == 5 else tile([P, R], F32, "buyer2_%d" % s)) for s in range(8)]
+
+        def w1_slice(s):
+            def operand(a):
                 c = 512 * a + P * (s % 4)
                 return w1_codes[s // 4][:, 2 * c : 2 * c + 2 * P].bitcast(FP4X4), planes[a][:, S + P * s : S + P * s + P]
 
-            window = first_stage(w1_slice, ACT.Square, None)
+            return operand
+
+        filled.extend(tile([P, S], F32, "window%d" % s) for s in range(2))
+        opened = {}
+        for s, j0, width, a in FIRST_PASSES:
+            first = (s, j0, width) not in opened
+            if first:
+                opened[s, j0, width] = next_bank()
+            multiply(opened[s, j0, width], w1_slice(s), j0, width, a, first)
+        for s, j0, width in sorted(opened):
+            empty(filled[s], j0, opened[s, j0, width][:, 0:width], ACT.Square)
+        for s in range(8):
+            window = filled[s] if s < 2 else first_stage(w1_slice(s), ACT.Square, None)
             nc.vector.tensor_copy(buyer2[s][:], window[:].indirect(p1[:]))
 
         def round_second_block(a):
@@ -209,7 +243,7 @@ def tile_list_refund_ring_links_kernel(
 
         round_second_block(0)
 
-        w3_raw = [placed([P, 4, N], F32, "w3_raw0", 0), tile([P, 4, N], F32, "w3_raw1", "w1_raw0")]
+        w3_raw = [placed([P, 4, N], F32, "w3_raw%d" % b, 10 * b) for b in range(2)]
         for b in range(2):
             nc.sync.dma_start(w3_raw[b][:], w3[512 * b : 512 * b + 512].rearrange("(p j) n -> p j n", j=4))
         w4_codes = tile([P, 2, N], U32, "w4_codes", "window4")
@@ -251,7 +285,7 @@ def tile_list_refund_ring_links_kernel(
             pick_device(0, t)
             if t == 1:
                 round_second_block(1)
-        w3_round = [placed([P, 2048], BF16, "w3_round%d" % b, 16 + 8 * b) for b in range(2)]
+        w3_round = [placed([P, 2048], BF16, "w3_round%d" % b, 18 + 8 * b) for b in range(2)]
         nc.vector.tensor_scalar_mul(woven(w3_round[0][:], 4), by_rows(w3_raw[0][:], 4), 0.5)
         nc.vector.tensor_scalar_mul(woven(w3_round[1][:, 0 : 4 * 384], 4), by_rows(w3_raw[1][:, :, 0:384], 4), 0.5)
         for t in range(4):
@@ -272,7 +306,7 @@ def tile_list_refund_ring_links_kernel(
 
         def regions(first_bank, width):
             per_bank = BANK // width
-            return [(banks[first_bank + n // per_bank], (n % per_bank) * width, n % per_bank) for n in range(4)]
+            return [(banks[(1 + first_bank + n // per_bank) % 8], (n % per_bank) * width, n % per_bank) for n in range(4)]
 
         def second_stage(b, zq, z0, width, gate_at, y_at):
             codes, scale = zq
@@ -313,10 +347,10 @@ def tile_list_refund_ring_links_kernel(
                 cols = slice(c0, c0 + 2 * width)
                 k = 2 * j * width // BANK
                 gate = tile([P, 2 * width], F32, "gate%d%d" % (i, j))
-                nc.scalar.activation(gate[:], banks[first + k][:, cols], ACT.Tanh, scale=0.5)
+                nc.scalar.activation(gate[:], banks[(1 + first + k) % 8][:, cols], ACT.Tanh, scale=0.5)
                 res = tile([P, 2 * width], F32, "res%d%d" % (i, j))
                 nc.vector.scalar_tensor_tensor(
-                    res[:], gate[:], 1.0, banks[first + count + k][:, cols], ALU.add, ALU.mult
+                    res[:], gate[:], 1.0, banks[(1 + first + count + k) % 8][:, cols], ALU.add, ALU.mult
                 )
                 (nc.scalar if (i, j) == (2, 0) else nc.sync).dma_start(
                     out_view[:, 2 * j : 2 * j + 2, m0 : m0 + width],

@@ -299,7 +299,7 @@ def tile_list_refund_ring_links_kernel(
         nc.scalar.activation(
             woven(w3_round[1][:, 4 * 384 : 4 * N], 4), by_rows(w3_raw[1][:, :, 384:N], 4), ACT.Copy, scale=0.5
         )
-        w3q.append(quantise(w3_round[1][:], N, "w3q1"))
+        w3q1 = [quantise(w3_round[1][:, 1024:2048], 256, "w3q11")]
         for m0, width in CHUNKS:
             for t in range(4):
                 pick_address(1, t, m0, width)
@@ -311,13 +311,17 @@ def tile_list_refund_ring_links_kernel(
         def second_stage(b, zq, z0, width, gate_at, y_at):
             codes, scale = zq
             per_bank = BANK // width
-            for places, weight in ((gate_at, 4), (y_at, 3)):
-                for n, (bank, c0, slot) in enumerate(places):
+            for n0, places, weight in [(n0, at, w) for n0 in reversed(range(0, 4, per_bank)) for at, w in ((gate_at, 4), (y_at, 3))]:
+                for n in range(n0, n0 + per_bank):
+                    bank, c0, slot = places[n]
                     cols = slice(P * n, P * n + P)
                     if weight == 4:
                         lhs, lhs_scale = w4_codes[:, b, cols], w4_scale[:, b, cols]
+                    elif b == 0:
+                        lhs, lhs_scale = w3q[0][0][:, cols], w3q[0][1][:, cols]
                     else:
-                        lhs, lhs_scale = w3q[b][0][:, cols], w3q[b][1][:, cols]
+                        codes3, scale3 = w3q1[1 - n // 2]
+                        lhs, lhs_scale = codes3[:, P * (n % 2) : P * (n % 2) + P], scale3[:, P * (n % 2) : P * (n % 2) + P]
                     nc.tensor.matmul_mx(
                         bank[:, c0 : c0 + width], lhsT=lhs.bitcast(FP8X4), lhsT_scale=lhs_scale,
                         rhs=codes[:, z0 : z0 + width].bitcast(FP8X4), rhs_scale=scale[:, z0 : z0 + width],
@@ -334,15 +338,17 @@ def tile_list_refund_ring_links_kernel(
             second_stage(0, zq0, m0, width, gate_at, y_at)
 
         z1_round = [round_z(1, m0, width, address[1, m0]) for m0, width in CHUNKS[:2]]
-        for i, ((m0, width), (first, count, gate_at, y_at)) in enumerate(zip(CHUNKS, places)):
-            if i == 1:
-                z1_round.append(round_z(1, *CHUNKS[2], address[1, CHUNKS[2][0]]))
-            zq = quantise(z1_round[i][:], width, "zq1%d" % i)
+        zq1 = [quantise(z1_round[0][:], CHUNKS[0][1], "zq10")]
+        z1_round.append(round_z(1, *CHUNKS[2], address[1, CHUNKS[2][0]]))
+        zq1.append(quantise(z1_round[1][:], CHUNKS[1][1], "zq11"))
+        w3q1.append(quantise(w3_round[1][:, 0:1024], 256, "w3q10", "window0"))
+        zq1.append(quantise(z1_round[2][:], CHUNKS[2][1], "zq12"))
+        for zq, (m0, width), (first, count, gate_at, y_at) in zip(zq1, CHUNKS, places):
             second_stage(1, zq, 0, width, gate_at, y_at)
 
         out_view = out.rearrange("(n p) m -> p n m", p=P)
         for i, ((m0, width), (first, count, gate_at, y_at)) in enumerate(zip(CHUNKS, places)):
-            for j in range(2):
+            for j in (1, 0):
                 c0 = (2 * j * width) % BANK
                 cols = slice(c0, c0 + 2 * width)
                 k = 2 * j * width // BANK
@@ -352,7 +358,7 @@ def tile_list_refund_ring_links_kernel(
                 nc.vector.scalar_tensor_tensor(
                     res[:], gate[:], 1.0, banks[(1 + first + count + k) % 8][:, cols], ALU.add, ALU.mult
                 )
-                (nc.scalar if (i, j) == (2, 0) else nc.sync).dma_start(
+                (nc.scalar if (i, j) == (2, 1) else nc.sync).dma_start(
                     out_view[:, 2 * j : 2 * j + 2, m0 : m0 + width],
                     res[:].rearrange("p (n m) -> p n m", m=width),
                 )

@@ -229,19 +229,22 @@ def tile_list_refund_ring_links_kernel(
             window = filled[s] if s < 2 else first_stage(w1_slice(s), ACT.Square, None)
             nc.vector.tensor_copy(buyer2[s][:], window[:].indirect(p1[:]))
 
-        def round_second_block(a):
-            rounded = tile([P, 2048], BF16, "w2_round1%d" % a, ("w2_round", "w2q00_codes")[a])
-            dst = rounded[:].rearrange("p (t m j) -> p m t j", t=4, j=4)
-            src = w2_raw1[a][:].rearrange("p j (m t) -> p m t j", t=4)
-            if a == 0:
-                nc.gpsimd.tensor_scalar(dst, src, 1.0, 0.0, ALU.mult, ALU.add)
-            else:
-                nc.scalar.activation(dst.rearrange("p m t j -> p m j t"), src.rearrange("p m t j -> p m j t"), ACT.Copy)
-            codes, scale = quantise(rounded[:], BANK, "w2q1%d" % a)
+        def quantise_second_block(a, rounded, codes):
+            scale = tile([P, BANK], U8, "w2q1%d_scale" % a)
+            nc.vector.quantize_mx(out=codes[:].bitcast(FP8X4), scales=scale[:], in_=rounded[:])
             for t in range(4):
                 w2q[1, t, a] = codes[:, P * t : P * t + P].bitcast(FP8X4), scale[:, P * t : P * t + P]
 
-        round_second_block(0)
+        w2_round1 = [tile([P, 2048], BF16, "w2_round1%d" % a, tag) for a, tag in enumerate(("w2_round", None))]
+        dst = [w2_round1[a][:].rearrange("p (t m j) -> p m t j", t=4, j=4) for a in range(2)]
+        src = [w2_raw1[a][:].rearrange("p j (m t) -> p m t j", t=4) for a in range(2)]
+        nc.gpsimd.tensor_scalar(dst[0], src[0], 1.0, 0.0, ALU.mult, ALU.add)
+        quantise_second_block(0, w2_round1[0], tile([P, BANK], U32, "w2q10_codes"))
+        for m0 in (0, 64):
+            nc.scalar.activation(
+                dst[1][:, m0 : m0 + 64].rearrange("p m t j -> p m j t"),
+                src[1][:, m0 : m0 + 64].rearrange("p m t j -> p m j t"), ACT.Copy,
+            )
 
         w3_raw = [placed([P, 4, N], F32, "w3_raw%d" % b, 10 * b) for b in range(2)]
         for b in range(2):
@@ -283,9 +286,9 @@ def tile_list_refund_ring_links_kernel(
         for t in range(4):
             link_slice(0, t)
             pick_device(0, t)
-            if t == 1:
-                round_second_block(1)
-        w3_round = [placed([P, 2048], BF16, "w3_round%d" % b, 18 + 8 * b) for b in range(2)]
+            if t == 0:
+                quantise_second_block(1, w2_round1[1], placed([P, BANK], U32, "w2q11_codes", 22))
+        w3_round = [placed([P, 2048], BF16, "w3_round%d" % b, 18 + 6 * b) for b in range(2)]
         nc.vector.tensor_scalar_mul(woven(w3_round[0][:], 4), by_rows(w3_raw[0][:], 4), 0.5)
         nc.vector.tensor_scalar_mul(woven(w3_round[1][:, 0 : 4 * 384], 4), by_rows(w3_raw[1][:, :, 0:384], 4), 0.5)
         for t in range(4):

@@ -298,14 +298,16 @@ def tile_list_refund_ring_links_kernel(
         for t in range(4):
             link_slice(1, t)
             pick_device(1, t)
-        zq0 = quantise(z0_round[:], R, "zq0")
-        nc.scalar.activation(
-            woven(w3_round[1][:, 4 * 384 : 4 * N], 4), by_rows(w3_raw[1][:, :, 384:N], 4), ACT.Copy, scale=0.5
-        )
-        w3q1 = [quantise(w3_round[1][:, 1024:2048], 256, "w3q11")]
+            if t == 1:
+                zq0 = quantise(z0_round[:], R, "zq0")
+        w3q1 = {0: quantise(w3_round[1][:, 0:1024], 256, "w3q10", "buyer2_6")}
         for m0, width in CHUNKS:
             for t in range(4):
                 pick_address(1, t, m0, width)
+            if m0 == 0:
+                nc.scalar.activation(
+                    woven(w3_round[1][:, 4 * 384 : 4 * N], 4), by_rows(w3_raw[1][:, :, 384:N], 4), ACT.Copy, scale=0.5
+                )
 
         def regions(first_bank, width):
             per_bank = BANK // width
@@ -323,7 +325,7 @@ def tile_list_refund_ring_links_kernel(
                     elif b == 0:
                         lhs, lhs_scale = w3q[0][0][:, cols], w3q[0][1][:, cols]
                     else:
-                        codes3, scale3 = w3q1[1 - n // 2]
+                        codes3, scale3 = w3q1[n // 2]
                         lhs, lhs_scale = codes3[:, P * (n % 2) : P * (n % 2) + P], scale3[:, P * (n % 2) : P * (n % 2) + P]
                     nc.tensor.matmul_mx(
                         bank[:, c0 : c0 + width], lhsT=lhs.bitcast(FP8X4), lhsT_scale=lhs_scale,
@@ -340,28 +342,35 @@ def tile_list_refund_ring_links_kernel(
         for (m0, width), (first, count, gate_at, y_at) in zip(CHUNKS, places):
             second_stage(0, zq0, m0, width, gate_at, y_at)
 
-        z1_round = [round_z(1, m0, width, address[1, m0]) for m0, width in CHUNKS[:2]]
-        zq1 = [quantise(z1_round[0][:], CHUNKS[0][1], "zq10")]
-        z1_round.append(round_z(1, *CHUNKS[2], address[1, CHUNKS[2][0]]))
-        zq1.append(quantise(z1_round[1][:], CHUNKS[1][1], "zq11"))
-        w3q1.append(quantise(w3_round[1][:, 0:1024], 256, "w3q10", "window0"))
-        zq1.append(quantise(z1_round[2][:], CHUNKS[2][1], "zq12"))
-        for zq, (m0, width), (first, count, gate_at, y_at) in zip(zq1, CHUNKS, places):
-            second_stage(1, zq, 0, width, gate_at, y_at)
-
         out_view = out.rearrange("(n p) m -> p n m", p=P)
-        for i, ((m0, width), (first, count, gate_at, y_at)) in enumerate(zip(CHUNKS, places)):
+
+        def finish(i, j):
+            (m0, width), (first, count, gate_at, y_at) = CHUNKS[i], places[i]
+            c0 = (2 * j * width) % BANK
+            cols = slice(c0, c0 + 2 * width)
+            k = 2 * j * width // BANK
+            gate = tile([P, 2 * width], F32, "gate%d%d" % (i, j))
+            nc.scalar.activation(gate[:], banks[(1 + first + k) % 8][:, cols], ACT.Tanh, scale=0.5)
+            res = tile([P, 2 * width], F32, "res%d%d" % (i, j))
+            nc.vector.scalar_tensor_tensor(
+                res[:], gate[:], 1.0, banks[(1 + first + count + k) % 8][:, cols], ALU.add, ALU.mult
+            )
+            (nc.scalar if (i, j) == (2, 1) else nc.sync).dma_start(
+                out_view[:, 2 * j : 2 * j + 2, m0 : m0 + width],
+                res[:].rearrange("p (n m) -> p n m", m=width),
+            )
+
+        z1_round = [round_z(1, *CHUNKS[0], address[1, 0])]
+        w3q1[1] = quantise(w3_round[1][:, 1024:2048], 256, "w3q11")
+        zq1 = [quantise(z1_round[0][:], CHUNKS[0][1], "zq10")]
+        second_stage(1, zq1[0], 0, CHUNKS[0][1], *places[0][2:])
+        z1_round.extend(round_z(1, m0, width, address[1, m0]) for m0, width in CHUNKS[1:])
+        zq1.append(quantise(z1_round[1][:], CHUNKS[1][1], "zq11"))
+        second_stage(1, zq1[1], 0, CHUNKS[1][1], *places[1][2:])
+        finish(0, 1)
+        zq1.append(quantise(z1_round[2][:], CHUNKS[2][1], "zq12"))
+        second_stage(1, zq1[2], 0, CHUNKS[2][1], *places[2][2:])
+        finish(0, 0)
+        for i in (1, 2):
             for j in (1, 0):
-                c0 = (2 * j * width) % BANK
-                cols = slice(c0, c0 + 2 * width)
-                k = 2 * j * width // BANK
-                gate = tile([P, 2 * width], F32, "gate%d%d" % (i, j))
-                nc.scalar.activation(gate[:], banks[(1 + first + k) % 8][:, cols], ACT.Tanh, scale=0.5)
-                res = tile([P, 2 * width], F32, "res%d%d" % (i, j))
-                nc.vector.scalar_tensor_tensor(
-                    res[:], gate[:], 1.0, banks[(1 + first + count + k) % 8][:, cols], ALU.add, ALU.mult
-                )
-                (nc.scalar if (i, j) == (2, 1) else nc.sync).dma_start(
-                    out_view[:, 2 * j : 2 * j + 2, m0 : m0 + width],
-                    res[:].rearrange("p (n m) -> p n m", m=width),
-                )
+                finish(i, j)

@@ -355,10 +355,14 @@ def tile_list_refund_ring_links_kernel(
             nc.vector.scalar_tensor_tensor(
                 res[:], gate[:], 1.0, banks[(1 + first + count + k) % 8][:, cols], ALU.add, ALU.mult
             )
-            (nc.scalar if (i, j) == (2, 1) else nc.sync).dma_start(
-                out_view[:, 2 * j : 2 * j + 2, m0 : m0 + width],
-                res[:].rearrange("p (n m) -> p n m", m=width),
-            )
+            if i < 2:
+                nc.sync.dma_start(
+                    out_view[:, 2 * j : 2 * j + 2, m0 : m0 + width],
+                    res[:].rearrange("p (n m) -> p n m", m=width),
+                )
+            else:
+                for k, queue in enumerate((nc.sync, nc.scalar)):
+                    queue.dma_start(out_view[:, 2 * j + k, m0 : m0 + width], res[:, k * width : k * width + width])
 
         z1_round = [round_z(1, *CHUNKS[0], address[1, 0])]
         w3q1[1] = quantise(w3_round[1][:, 1024:2048], 256, "w3q11")

@@ -355,13 +355,13 @@ def tile_list_refund_ring_links_kernel(
             nc.vector.scalar_tensor_tensor(
                 res[:], gate[:], 1.0, banks[(1 + first + count + k) % 8][:, cols], ALU.add, ALU.mult
             )
-            if i < 2:
+            if i == 1:
                 nc.sync.dma_start(
                     out_view[:, 2 * j : 2 * j + 2, m0 : m0 + width],
                     res[:].rearrange("p (n m) -> p n m", m=width),
                 )
             else:
-                for k, queue in enumerate((nc.sync, nc.scalar)):
+                for k, queue in enumerate((nc.sync, nc.scalar if i else nc.sync)):
                     queue.dma_start(out_view[:, 2 * j + k, m0 : m0 + width], res[:, k * width : k * width + width])
 
         z1_round = [round_z(1, *CHUNKS[0], address[1, 0])]

@@ -79,10 +79,10 @@ def tile_list_refund_ring_links_kernel(
         )
         table = [load_table(0)]
         load_w1(0, "w1_raw0")
+        table.append(load_table(1))
         p1 = load_list("p1", pos1, R)
         p2 = load_list("p2", pos2, R)
         p3 = load_list("p3", pos3, R)
-        table.append(load_table(1))
 
         for rows in (ts_rows, w1s_rows):
             nc.vector.memset(rows[32:64, :].bitcast(I32), 0)

from contextlib import ExitStack

import concourse.mybir as mybir

K, H, N, T, S, R = 1024, 1024, 512, 4096, 1024, 512
FLOPS = 2 * (2 * K * H * S + 2 * H * N * R)

F32 = mybir.dt.float32
BF16 = mybir.dt.bfloat16
I32 = mybir.dt.int32
U32 = mybir.dt.uint32
U16 = mybir.dt.uint16
U8 = mybir.dt.uint8
FP8X4 = mybir.dt.float8_e4m3fn_x4
FP4X4 = mybir.dt.float4_e2m1fn_x4
ACT = mybir.ActivationFunctionType
ALU = mybir.AluOpType

P = 128
BANK = 512
FIRST_PASSES = (
    (0, 0, 512, 0), (0, 512, 256, 0), (0, 768, 256, 0), (0, 0, 512, 1), (0, 512, 256, 1),
    (1, 0, 512, 1), (0, 768, 256, 1), (1, 0, 512, 0), (1, 512, 512, 1), (1, 512, 512, 0),
)
CHUNKS = ((0, 256), (256, 128), (384, 128))


def tile_list_refund_ring_links_kernel(
    tc, tab_words, tab_scales, offs, w1_words, w1_scales, w2, pos1, pos2, pos3, w3, w4_words, w4_scales, out
):
    nc = tc.nc
    with ExitStack() as ctx:
        lists = ctx.enter_context(tc.tile_pool(name="lists", bufs=1))
        sb = ctx.enter_context(tc.tile_pool(name="sb", bufs=1))
        reused = ctx.enter_context(tc.tile_pool(name="reused", bufs=1))
        psum = ctx.enter_context(tc.psum_pool(name="psum", bufs=1))

        def tile(shape, dtype, name, tag=None):
            return sb.tile(shape, dtype, name=name, tag=tag or name, align_bytes=64)

        def placed(shape, dtype, name, kib):
            return reused.tile(shape, dtype, name=name, tag=name, offset=1024 * kib, align_bytes=64)

        banks = [psum.tile([P, BANK], F32, name="bank%d" % i) for i in range(8)]

        def load_list(name, src, entries):
            offsets = lists.tile([P, entries // 16], U16, name=name)
            nc.sync.dma_start(offsets[:], src)
            return offsets

        def load_table(a):
            words = placed([P, T], U32, "table%d" % a, 2 + 16 * a)
            nc.sync.dma_start(
                words[:].bitcast(I32), tab_words[a].rearrange("p t i -> p (t i)").bitcast(I32)
            )
            return words

        def load_w2(b, a, dst):
            rows = w2[512 * a : 512 * a + 512, 512 * b : 512 * b + 512]
            nc.sync.dma_start(dst, rows.rearrange("(p j) c -> p j c", j=4))

        w1_raw = {}

        def load_w1(b, tag):
            w1_raw[b] = tile([P, 2, 256], U32, "w1_raw%d" % b, tag)
            nc.sync.dma_start(
                w1_raw[b][:].bitcast(I32),
                w1_words[:, :, 1024 * b : 1024 * b + 1024].rearrange("a p c -> p a c").bitcast(I32),
            )

        idx = load_list("idx", offs, S)
        ts_rows = tile([P, T], U8, "ts_rows")
        nc.sync.dma_start(
            ts_rows[0:32, :].bitcast(I32), tab_scales.rearrange("a q t -> (a q) t").bitcast(I32)
        )
        w1s_rows = tile([P, H], U8, "w1s_rows")
        nc.sync.dma_start(
            w1s_rows[0:32, :].bitcast(I32), w1_scales.rearrange("a q c -> (a q) c").bitcast(I32)
        )
        table = [load_table(0)]
        load_w1(0, "w1_raw0")
        table.append(load_table(1))
        p1 = load_list("p1", pos1, R)
        p2 = load_list("p2", pos2, R)
        p3 = load_list("p3", pos3, R)

        for rows in (ts_rows, w1s_rows):
            nc.vector.memset(rows[32:64, :].bitcast(I32), 0)
            nc.vector.memset(rows[64:128, :].bitcast(I32), 0)
        planes = [tile([P, S + H], U8, "planes%d" % a) for a in range(2)]
        nc.vector.memset(planes[1][:].bitcast(I32), 0)

        scale_rows = planes[0]
        nc.vector.tensor_copy(
            scale_rows[:, S : S + H].rearrange("p (b t m) -> p b t m", t=4, m=P),
            w1s_rows[:].rearrange("p (b m t) -> p b t m", t=4, m=P),
        )
        ts_picked = tile([P, S], U8, "ts_picked")
        nc.vector.tensor_copy(ts_picked[:], ts_rows[:].indirect(idx[:]))
        nc.vector.tensor_copy(scale_rows[:, 0:S].bitcast(I32), ts_picked[:].bitcast(I32))
        for a in (0, 1):
            for q in range(1 - a, 4):
                nc.sync.dma_start(
                    planes[a][32 * q : 32 * q + 4, :].bitcast(I32),
                    scale_rows[16 * a + 4 * q : 16 * a + 4 * q + 4, :].bitcast(I32),
                )

        load_w1(1, "ts_picked")
        v_words = [[tile([P, BANK], U32, "v_words%d%d" % (a, h)) for h in range(2)] for a in range(2)]

        def pick_words(a):
            for j0, width in ((0, 512), (512, 512)) if a == 0 else ((0, 512), (512, 256), (768, 256)):
                nc.vector.tensor_copy(
                    v_words[a][j0 // BANK][:, j0 % BANK : j0 % BANK + width],
                    table[a][:].indirect(idx[:, j0 // 16 : (j0 + width) // 16]),
                )

        w1_codes = {}

        def order_w1(b):
            w1_codes[b] = tile([P, 2048], U8, "w1_codes%d" % b)
            nc.vector.tensor_copy(
                w1_codes[b][:].bitcast(U16).rearrange("p (a t m) -> p a t m", t=4, m=P),
                w1_raw[b][:].rearrange("p a c -> p (a c)").bitcast(U16).rearrange("p (a m t) -> p a t m", t=4, m=P),
            )

        pick_words(0)
        order_w1(0)
        for i in range(5):
            nc.tensor.matmul_mx(
                banks[7][:], lhsT=w1_codes[0][:, 0 : 2 * P].bitcast(FP4X4), lhsT_scale=w1s_rows[:, 0:P],
                rhs=v_words[0][0][:].bitcast(FP8X4), rhs_scale=w1s_rows[:, 0:BANK], start=True, stop=True,
            )
        pick_words(1)
        order_w1(1)

        w2_raw00 = [placed([P, 4, 256], F32, "w2_raw00%d" % half, 4 * half) for half in range(2)]
        for half in range(2):
            rows = w2[0:512, 256 * half : 256 * half + 256]
            nc.sync.dma_start(w2_raw00[half][:], rows.rearrange("(p j) c -> p j c", j=4))
        w2_raw01 = placed([P, 4, 512], F32, "w2_raw01", 8)
        load_w2(0, 1, w2_raw01[:])
        w2_raw1 = [placed([P, 4, 512], F32, "w2_raw1%d" % a, 18 + 8 * a) for a in range(2)]
        for a in range(2):
            load_w2(1, a, w2_raw1[a][:])

        filled = []

        used = []

        def next_bank():
            used.append(banks[len(used) % 8])
            return used[-1]

        def multiply(bank, lhs, j0, width, a, first):
            codes, scale = lhs(a)
            nc.tensor.matmul_mx(
                bank[:, 0:width], lhsT=codes, lhsT_scale=scale,
                rhs=v_words[a][j0 // BANK][:, j0 % BANK : j0 % BANK + width].bitcast(FP8X4),
                rhs_scale=planes[a][:, j0 : j0 + width],
                start=first, stop=not first,
            )

        def empty(window, j0, sums, func):
            dst = window[:, j0 : j0 + sums.shape[1]]
            if func == ACT.Copy:
                nc.scalar.copy(dst, sums)
            else:
                nc.scalar.activation(dst, sums, func)

        def first_stage(lhs, func, tag):
            window = tile([P, S], F32, "window%d" % len(filled), tag)
            for j0 in (0, BANK):
                bank = next_bank()
                for a in (1, 0):
                    multiply(bank, lhs, j0, BANK, a, a == 1)
                empty(window, j0, bank[:], func)
            filled.append(window)
            return window

        def quantise(rounded, width, name, tag=None):
            codes = tile([P, width], U32, name + "_codes", tag)
            scale = tile([P, width], U8, name + "_scale")
            nc.vector.quantize_mx(out=codes[:].bitcast(FP8X4), scales=scale[:], in_=rounded)
            return codes, scale

        def woven(dst, run):
            return dst.rearrange("p (c i j) -> p c j i", i=run, j=4)

        def by_rows(src, run):
            return src.rearrange("p j (c i) -> p c j i", i=run)

        w2q = {}

        def round_w2(b, pieces):
            rounded = tile([P, 4096], BF16, "w2_round%d" % b, "w2_round")
            dst = rounded[:].rearrange("p (t a m j) -> p a m t j", t=4, a=2, j=4)
            for a, m0, raw in pieces:
                src = raw.rearrange("p j (m t) -> p m t j", t=4)
                nc.gpsimd.tensor_scalar(dst[:, a, m0 : m0 + src.shape[1]], src, 1.0, 0.0, ALU.mult, ALU.add)
            for pair in range(2):
                codes, scale = quantise(rounded[:, 2048 * pair : 2048 * pair + 2048], BANK, "w2q%d%d" % (b, pair))
                for t in range(2):
                    for a in range(2):
                        cols = slice(P * (2 * t + a), P * (2 * t + a) + P)
                        w2q[b, 2 * pair + t, a] = codes[:, cols].bitcast(FP8X4), scale[:, cols]

        round_w2(0, [(0, 0, w2_raw00[0][:]), (0, 64, w2_raw00[1][:]), (1, 0, w2_raw01[:])])

        buyer2 = [(placed([P, R], F32, "buyer2_5", 8) if s == 5 else tile([P, R], F32, "buyer2_%d" % s)) for s in range(8)]

        def w1_slice(s):
            def operand(a):
                c = 512 * a + P * (s % 4)
                return w1_codes[s // 4][:, 2 * c : 2 * c + 2 * P].bitcast(FP4X4), planes[a][:, S + P * s : S + P * s + P]

            return operand

        filled.extend(tile([P, S], F32, "window%d" % s) for s in range(2))
        opened = {}
        for s, j0, width, a in FIRST_PASSES:
            first = (s, j0, width) not in opened
            if first:
                opened[s, j0, width] = next_bank()
            multiply(opened[s, j0, width], w1_slice(s), j0, width, a, first)
        for s, j0, width in sorted(opened):
            empty(filled[s], j0, opened[s, j0, width][:, 0:width], ACT.Square)
        for s in range(8):
            window = filled[s] if s < 2 else first_stage(w1_slice(s), ACT.Square, None)
            nc.vector.tensor_copy(buyer2[s][:], window[:].indirect(p1[:]))

        def quantise_second_block(a, rounded, codes):
            scale = tile([P, BANK], U8, "w2q1%d_scale" % a)
            nc.vector.quantize_mx(out=codes[:].bitcast(FP8X4), scales=scale[:], in_=rounded[:])
            for t in range(4):
                w2q[1, t, a] = codes[:, P * t : P * t + P].bitcast(FP8X4), scale[:, P * t : P * t + P]

        w2_round1 = [tile([P, 2048], BF16, "w2_round1%d" % a, tag) for a, tag in enumerate(("w2_round", None))]
        dst = [w2_round1[a][:].rearrange("p (t m j) -> p m t j", t=4, j=4) for a in range(2)]
        src = [w2_raw1[a][:].rearrange("p j (m t) -> p m t j", t=4) for a in range(2)]
        nc.gpsimd.tensor_scalar(dst[0], src[0], 1.0, 0.0, ALU.mult, ALU.add)
        quantise_second_block(0, w2_round1[0], tile([P, BANK], U32, "w2q10_codes"))
        for m0 in (0, 64):
            nc.scalar.activation(
                dst[1][:, m0 : m0 + 64].rearrange("p m t j -> p m j t"),
                src[1][:, m0 : m0 + 64].rearrange("p m t j -> p m j t"), ACT.Copy,
            )

        w3_raw = [placed([P, 4, N], F32, "w3_raw%d" % b, 10 * b) for b in range(2)]
        for b in range(2):
            nc.sync.dma_start(w3_raw[b][:], w3[512 * b : 512 * b + 512].rearrange("(p j) n -> p j n", j=4))
        w4_codes = tile([P, 2, N], U32, "w4_codes", "window4")
        nc.sync.dma_start(w4_codes[:].bitcast(I32), w4_words.rearrange("b p c i -> p b (c i)").bitcast(I32))
        w4_scale = planes[1][:, S : S + 2 * N].rearrange("p (b c) -> p b c", b=2)
        for q in range(4):
            nc.sync.dma_start(
                w4_scale[32 * q : 32 * q + 4].bitcast(I32),
                w4_scales[:, 4 * q : 4 * q + 4, :].rearrange("b r c -> r b c").bitcast(I32),
            )

        link = {}
        prod = [tile([P, 4, R], F32, "prod%d" % b) for b in range(2)]

        def link_slice(b, t):
            link[b, t] = first_stage(lambda a: w2q[b, t, a], ACT.Copy, ("window%d" % t) if b else None)

        def pick_device(b, t):
            nc.vector.tensor_tensor(prod[b][:, t, :], link[b, t][:].indirect(p2[:]), buyer2[4 * b + t][:], ALU.mult)

        address = {}

        def pick_address(b, t, m0, width):
            if (b, m0) not in address:
                address[b, m0] = tile([P, 4, width], F32, "address%d_%d" % (b, m0))
            nc.scalar.activation(
                address[b, m0][:, t, :], link[b, t][:].indirect(p3[:, m0 // 16 : (m0 + width) // 16]), ACT.Copy
            )

        def round_z(b, m0, width, address):
            rounded = tile([P, 4 * width], BF16, "z_round%d_%d" % (b, m0))
            nc.vector.tensor_tensor(
                woven(rounded[:], 2), by_rows(prod[b][:, :, m0 : m0 + width], 2), by_rows(address[:], 2), ALU.subtract
            )
            return rounded

        for t in range(4):
            link_slice(0, t)
            pick_device(0, t)
            if t == 0:
                quantise_second_block(1, w2_round1[1], placed([P, BANK], U32, "w2q11_codes", 22))
        w3_round = [placed([P, 2048], BF16, "w3_round%d" % b, 18 + 6 * b) for b in range(2)]
        nc.vector.tensor_scalar_mul(woven(w3_round[0][:], 4), by_rows(w3_raw[0][:], 4), 0.5)
        nc.vector.tensor_scalar_mul(woven(w3_round[1][:, 0 : 4 * 384], 4), by_rows(w3_raw[1][:, :, 0:384], 4), 0.5)
        for t in range(4):
            pick_address(0, t, 0, R)
        w3q = [quantise(w3_round[0][:], N, "w3q0", "window8")]
        z0_round = round_z(0, 0, R, address[0, 0])
        for t in range(4):
            link_slice(1, t)
            pick_device(1, t)
            if t == 1:
                zq0 = quantise(z0_round[:], R, "zq0")
        w3q1 = {0: quantise(w3_round[1][:, 0:1024], 256, "w3q10", "buyer2_6")}
        for m0, width in CHUNKS:
            for t in range(4):
                pick_address(1, t, m0, width)
            if m0 == 0:
                nc.scalar.activation(
                    woven(w3_round[1][:, 4 * 384 : 4 * N], 4), by_rows(w3_raw[1][:, :, 384:N], 4), ACT.Copy, scale=0.5
                )

        def regions(first_bank, width):
            per_bank = BANK // width
            return [(banks[(1 + first_bank + n // per_bank) % 8], (n % per_bank) * width, n % per_bank) for n in range(4)]

        def second_stage(b, zq, z0, width, gate_at, y_at):
            codes, scale = zq
            per_bank = BANK // width
            for n0, places, weight in [(n0, at, w) for n0 in reversed(range(0, 4, per_bank)) for at, w in ((gate_at, 4), (y_at, 3))]:
                for n in range(n0, n0 + per_bank):
                    bank, c0, slot = places[n]
                    cols = slice(P * n, P * n + P)
                    if weight == 4:
                        lhs, lhs_scale = w4_codes[:, b, cols], w4_scale[:, b, cols]
                    elif b == 0:
                        lhs, lhs_scale = w3q[0][0][:, cols], w3q[0][1][:, cols]
                    else:
                        codes3, scale3 = w3q1[n // 2]
                        lhs, lhs_scale = codes3[:, P * (n % 2) : P * (n % 2) + P], scale3[:, P * (n % 2) : P * (n % 2) + P]
                    nc.tensor.matmul_mx(
                        bank[:, c0 : c0 + width], lhsT=lhs.bitcast(FP8X4), lhsT_scale=lhs_scale,
                        rhs=codes[:, z0 : z0 + width].bitcast(FP8X4), rhs_scale=scale[:, z0 : z0 + width],
                        start=(b == 0 and slot == 0), stop=(b == 1 and slot == per_bank - 1),
                    )

        places = []
        first = 0
        for m0, width in CHUNKS:
            count = 4 * width // BANK
            places.append((first, count, regions(first, width), regions(first + count, width)))
            first += 2 * count
        for (m0, width), (first, count, gate_at, y_at) in zip(CHUNKS, places):
            second_stage(0, zq0, m0, width, gate_at, y_at)

        out_view = out.rearrange("(n p) m -> p n m", p=P)

        def finish(i, j):
            (m0, width), (first, count, gate_at, y_at) = CHUNKS[i], places[i]
            c0 = (2 * j * width) % BANK
            cols = slice(c0, c0 + 2 * width)
            k = 2 * j * width // BANK
            gate = tile([P, 2 * width], F32, "gate%d%d" % (i, j))
            nc.scalar.activation(gate[:], banks[(1 + first + k) % 8][:, cols], ACT.Tanh, scale=0.5)
            res = tile([P, 2 * width], F32, "res%d%d" % (i, j))
            nc.vector.scalar_tensor_tensor(
                res[:], gate[:], 1.0, banks[(1 + first + count + k) % 8][:, cols], ALU.add, ALU.mult
            )
            if i == 1:
                nc.sync.dma_start(
                    out_view[:, 2 * j : 2 * j + 2, m0 : m0 + width],
                    res[:].rearrange("p (n m) -> p n m", m=width),
                )
            else:
                for k, queue in enumerate((nc.sync, nc.scalar if i else nc.sync)):
                    queue.dma_start(out_view[:, 2 * j + k, m0 : m0 + width], res[:, k * width : k * width + width])

        z1_round = [round_z(1, *CHUNKS[0], address[1, 0])]
        w3q1[1] = quantise(w3_round[1][:, 1024:2048], 256, "w3q11")
        zq1 = [quantise(z1_round[0][:], CHUNKS[0][1], "zq10")]
        second_stage(1, zq1[0], 0, CHUNKS[0][1], *places[0][2:])
        z1_round.extend(round_z(1, m0, width, address[1, m0]) for m0, width in CHUNKS[1:])
        zq1.append(quantise(z1_round[1][:], CHUNKS[1][1], "zq11"))
        second_stage(1, zq1[1], 0, CHUNKS[1][1], *places[1][2:])
        finish(0, 1)
        zq1.append(quantise(z1_round[2][:], CHUNKS[2][1], "zq12"))
        second_stage(1, zq1[2], 0, CHUNKS[2][1], *places[2][2:])
        finish(0, 0)
        for i in (1, 2):
            for j in (1, 0):
                finish(i, j)
